import numpy as np
import ml_dtypes


def mxq(x, axis, fmt="e4m3"):
    dtype, down = {"e4m3": (ml_dtypes.float8_e4m3fn, 7), "e5m2": (ml_dtypes.float8_e5m2, 14)}[fmt]
    v = np.moveaxis(np.asarray(x, np.float32).astype(ml_dtypes.bfloat16).astype(np.float64), axis, -1)
    blocks = v.reshape(v.shape[:-1] + (-1, 32))
    amax = np.abs(blocks).max(-1, keepdims=True)
    byte = np.maximum(np.where(amax > 0, np.frexp(amax)[1] - 1 + 127, 0) - down, 1)
    scale = np.exp2(byte - 127.0)
    codes = (blocks / scale).astype(np.float32).astype(dtype).astype(np.float64)
    return np.moveaxis((codes * scale).reshape(v.shape), -1, axis)


WIDE = False


def mx_kscale(k):
    if not WIDE:
        return np.ones(k)
    levels = np.array([10, -10, 5, -5, 0])
    if k % 512:
        return np.exp2(np.random.permutation(np.resize(levels, k // 32))).repeat(32)
    a = np.empty((k // 512, 16))
    for p in range(k // 512):
        a[p, :8] = np.random.permutation(np.resize(levels, 8))
        for g in range(8):
            far = levels[np.abs(levels - a[p, g]) >= 10]
            a[p, g + 8] = far[np.random.randint(len(far))]
    return np.exp2(a.ravel()).repeat(32)


def f64(x):
    return np.asarray(x).astype(np.float64)


def striped(idx):
    return np.tile(idx.reshape(-1, 16).T, (8, 1)).astype(np.uint16)


def unstriped(offs):
    return offs[:16].T.reshape(-1).astype(np.int64)


E2M1 = np.array([0.0, 0.5, 1.0, 1.5, 2.0, 3.0, 4.0, 6.0, -0.0, -0.5, -1.0, -1.5, -2.0, -3.0, -4.0, -6.0])


def pack_weight(w, fmt):
    k, n = w.shape
    w = f64(np.asarray(w, np.float32).astype(ml_dtypes.bfloat16)).reshape(k // 32, 32, n)
    amax = np.abs(w).max(1)
    if fmt == "e4m3":
        byte = np.frexp(amax)[1] - 1 + 127 - 7
    else:
        mant, ex = np.frexp(amax / 6.0)
        byte = np.where(mant > 0.5, ex, ex - 1) + 127
    byte = np.clip(np.where(amax > 0, byte, 1), 1, 254)
    scaled = (w * np.exp2(127.0 - byte)[:, None, :]).reshape(k, n).astype(np.float32)
    by_word = np.ascontiguousarray(scaled.reshape(k // 512, 128, 4, n).transpose(0, 1, 3, 2))
    if fmt == "e4m3":
        words = by_word.astype(ml_dtypes.float8_e4m3fn).view(np.uint8)
    else:
        c = by_word.astype(ml_dtypes.float4_e2m1fn).view(np.uint8) & 0xF
        words = (c[..., 0::2] | (c[..., 1::2] << 4)).reshape(k // 512, 128, 2 * n)
    return np.ascontiguousarray(words), np.ascontiguousarray(byte.astype(np.uint8).reshape(k // 512, 16, n))


def unpack_weight(words, scales, fmt):
    g, _, n = scales.shape
    words = np.ascontiguousarray(words).reshape(g, 128, n, -1)
    if fmt == "e4m3":
        vals = words.view(ml_dtypes.float8_e4m3fn).astype(np.float64)
    else:
        nib = np.empty((g, 128, n, 4), np.uint8)
        nib[..., 0::2] = words & 0xF
        nib[..., 1::2] = words >> 4
        vals = E2M1[nib]
    vals = vals * np.repeat(np.exp2(scales.astype(np.float64) - 127.0), 8, axis=1)[..., None]
    return vals.transpose(0, 1, 3, 2).reshape(g * 512, n)


def silu(v):
    return v / (1.0 + np.exp(-np.maximum(v, -700.0)))


K, T, Q, E, C, D, H = 512, 1024, 768, 6, 128, 128, 0
N = 512


def by_expert(wq, xq, C):
    return np.concatenate([wq[e].T @ xq[:, e * C:(e + 1) * C] for e in range(E)], axis=1)


def setup_inputs():
    n = np.random.standard_normal
    s = mx_kscale(K)
    slot_token = np.random.permutation(T)[:E * C]
    slots2 = np.concatenate([np.random.permutation(Q)[:D] for e in range(E)])
    x = pack_weight(n((K, Q)) * s[:, None], "e4m3")
    w = [pack_weight(m, "e2m1") for m in n((E, K, N)) / np.sqrt(K) / s[None, :, None]]
    return {
        "x_words": x[0],
        "x_scales": x[1],
        "xo": (n((K, T)) * s[:, None]).astype(np.float32),
        "w_words": np.stack([m[0] for m in w]),
        "w_scales": np.stack([m[1] for m in w]),
        "gate": np.tile(np.random.uniform(0.2, 1.0, E * C), (128, 1)).astype(np.float32),
        "offs": striped(slot_token),
        "offs2": striped(slots2),
    }


def reference(x_words, x_scales, xo, w_words, w_scales, gate, offs, offs2):
    w = np.stack([unpack_weight(w_words[e], w_scales[e], "e2m1") for e in range(E)])
    idx, idx2 = unstriped(offs), unstriped(offs2)
    xq = mxq(f64(xo)[:, idx], 0, "e4m3")
    rq = unpack_weight(x_words, x_scales, "e4m3")[:, idx2]
    y = silu(by_expert(w, xq, C))
    z = silu(by_expert(w, rq, D))
    own = np.zeros((N, T))
    own[:, idx] = f64(gate[:1]) * y
    return np.concatenate([own, z], axis=1)

@@ -1,0 +1,200 @@
+from contextlib import ExitStack
+
+import concourse.mybir as mybir
+
+K, T, Q, E, C, N = 512, 1024, 768, 6, 128, 512
+S = E * C
+FLOPS = 2 * K * N * 2 * S
+
+F32 = mybir.dt.float32
+BF16 = mybir.dt.bfloat16
+I32 = mybir.dt.int32
+U32 = mybir.dt.uint32
+U16 = mybir.dt.uint16
+U8 = mybir.dt.uint8
+FP8X4 = mybir.dt.float8_e4m3fn_x4
+FP4X4 = mybir.dt.float4_e2m1fn_x4
+SILU = mybir.ActivationFunctionType.Silu
+COPY = mybir.ActivationFunctionType.Copy
+MULT = mybir.AluOpType.mult
+
+P = 128
+PACK = 4
+NB = N // P
+HALF = S // 2
+EARLY = 2
+
+
+def tile_moe_loc_lin_silu_kernel(
+    tc, x_words, x_scales, xo, w_words, w_scales, gate, offs, offs2, out
+):
+    nc = tc.nc
+    with ExitStack() as ctx:
+        keep = ctx.enter_context(tc.tile_pool(name="keep", bufs=1))
+        psum = ctx.enter_context(tc.psum_pool(name="psum", bufs=8))
+
+        own_list = keep.tile([P, S // 16], U16, name="own_list")
+        far_list = keep.tile([P, S // 16], U16, name="far_list")
+        far_words = keep.tile([P, Q], I32, name="far_words", align_bytes=64)
+        far_bytes = keep.tile([P, Q], U8, name="far_bytes", align_bytes=64)
+        xf = [keep.tile([P, T], F32, name=f"xf{j}", align_bytes=64) for j in range(PACK)]
+        xb = [keep.tile([P, T], BF16, name=f"xb{j}", align_bytes=64) for j in range(PACK)]
+        spans = [(0, EARLY), (EARLY, E)]
+        ww = [keep.tile([P, b - a, 2 * N], U8, name=f"ww{a}", align_bytes=64) for a, b in spans]
+        ws = [keep.tile([P, b - a, N], U8, name=f"ws{a}", align_bytes=64) for a, b in spans]
+        gates = keep.tile([P, S], F32, name="gates", align_bytes=64)
+        win = [keep.tile([P, T], F32, name=f"win{nb}", align_bytes=64) for nb in range(NB)]
+
+        nc.vector.memset(far_bytes[:].bitcast(I32), 0)
+        for t in ws:
+            nc.vector.memset(t[:].rearrange("p e n -> p (e n)").bitcast(I32), 0)
+        for nb in range(NB - 1):
+            nc.vector.memset(win[nb][:], 0.0)
+        nc.scalar.activation(win[NB - 1][:], win[0][:], SILU)
+
+        def load_weights(i):
+            a, b = spans[i]
+            for r in range(4):
+                nc.sync.dma_start(
+                    out=ws[i][r:P:32, :, :].bitcast(I32),
+                    in_=w_scales[a:b, 0, r:16:4, :].rearrange("e q n -> q e n").bitcast(I32),
+                )
+            nc.sync.dma_start(
+                out=ww[i][:].bitcast(I32),
+                in_=w_words[a:b, 0, :, :].rearrange("e p b -> p e b").bitcast(I32),
+            )
+
+        xo_planes = xo.rearrange("(p j) t -> p j t", j=PACK)
+        nc.sync.dma_start(far_list[:], offs2)
+        nc.sync.dma_start(out=far_words[:], in_=x_words[0].rearrange("p t d -> p (t d)").bitcast(I32))
+        for r in range(4):
+            nc.sync.dma_start(out=far_bytes[r:P:32, :].bitcast(I32), in_=x_scales[0, r:16:4, :].bitcast(I32))
+        nc.sync.dma_start(out=xf[0][:], in_=xo_planes[:, 0, :])
+        nc.sync.dma_start(own_list[:], offs)
+        for j in range(1, PACK):
+            nc.sync.dma_start(out=xf[j][:], in_=xo_planes[:, j, :])
+        load_weights(0)
+        nc.sync.dma_start(out=gates[:], in_=gate)
+        load_weights(1)
+
+        def weights(e, nb):
+            i = 0 if e < EARLY else 1
+            le = e - spans[i][0]
+            return (
+                ww[i][:, le, 2 * P * nb : 2 * P * (nb + 1)].bitcast(FP4X4),
+                ws[i][:, le, P * nb : P * (nb + 1)],
+            )
+
+        def multiply(dst, e, nb, codes, scales):
+            w, s = weights(e, nb)
+            nc.tensor.matmul_mx(
+                out=dst, lhsT=w, lhsT_scale=s, rhs=codes.bitcast(FP8X4), rhs_scale=scales, start=True, stop=True
+            )
+
+        far_codes = [keep.tile([P, HALF], U32, name=f"far_codes{h}", align_bytes=64) for h in range(2)]
+        far_scales = [keep.tile([P, HALF], U8, name=f"far_scales{h}", align_bytes=64) for h in range(2)]
+
+        def far_cols(h):
+            return far_list[:, h * HALF // 16 : (h + 1) * HALF // 16]
+
+        def gather_far_words(h):
+            nc.vector.tensor_copy(far_codes[h][:], far_words[:].bitcast(U32).indirect(far_cols(h)))
+
+        def gather_far_bytes(h):
+            nc.vector.tensor_copy(far_scales[h][:], far_bytes[:].indirect(far_cols(h)))
+
+        groups = [(0, 128), (128, 128), (256, 256), (512, 256)]
+        rows = [keep.tile([P, n, PACK], BF16, name=f"rows{s}", align_bytes=64) for s, n in groups]
+        codes = [keep.tile([P, n], U32, name=f"codes{s}", align_bytes=64) for s, n in groups]
+        scales = [keep.tile([P, n], U8, name=f"scales{s}", align_bytes=64) for s, n in groups]
+        ys = [[keep.tile([P, n], F32, name=f"y{s}_{nb}", align_bytes=64) for nb in range(NB)] for s, n in groups[:1]]
+        yw = [None] + [keep.tile([P, NB, n], F32, name=f"yw{s}", align_bytes=64) for s, n in groups[1:]]
+        zs = [keep.tile([P, NB, HALF], F32, name=f"z{h}", align_bytes=64) for h in range(2)]
+
+        def own_cols(g):
+            s, n = groups[g]
+            return own_list[:, s // 16 : (s + n) // 16]
+
+        def gather_vector(g, j):
+            nc.vector.tensor_copy(rows[g][:, :, j], xf[j][:].indirect(own_cols(g)))
+
+        def gather_scalar(g, j):
+            nc.scalar.activation(rows[g][:, :, j], xb[j][:].indirect(own_cols(g)), COPY)
+
+        def quantize(g):
+            nc.vector.quantize_mx(
+                out=codes[g][:].bitcast(FP8X4), scales=scales[g][:], in_=rows[g][:].rearrange("p n j -> p (n j)")
+            )
+
+        def result(g, nb):
+            return ys[0][nb][:] if g == 0 else yw[g][:, nb, :]
+
+        def experts(g):
+            s, n = groups[g]
+            per_bank = 1 if g == 0 else 512 // n
+            for nb0 in range(0, NB, per_bank):
+                bank = psum.tile([P, per_bank, n], F32, name="bank")
+                for i in range(per_bank):
+                    for u in range(n // C):
+                        cols = slice(u * C, (u + 1) * C)
+                        multiply(bank[:, i, cols], s // C + u, nb0 + i, codes[g][:, cols], scales[g][:, cols])
+                if g == 0:
+                    nc.scalar.activation(ys[0][nb0][:], bank[:, 0, :], SILU)
+                else:
+                    nc.scalar.activation(yw[g][:, nb0 : nb0 + per_bank, :], bank[:], SILU)
+
+        def scatter(g, nb):
+            s, n = groups[g]
+            nc.vector.tensor_tensor(win[nb][:].indirect(own_cols(g)), result(g, nb), gates[:, s : s + n], MULT)
+
+        def far_expert(e):
+            h, u = divmod(e, E // 2)
+            cols = slice(u * C, (u + 1) * C)
+            bank = psum.tile([P, NB, C], F32, name="bank")
+            for nb in range(NB):
+                multiply(bank[:, nb, :], e, nb, far_codes[h][:, cols], far_scales[h][:, cols])
+            nc.scalar.activation(zs[h][:, :, cols], bank[:], SILU)
+
+        out_rows = out.rearrange("(nb p) t -> p nb t", p=P)
+
+        gather_far_words(0)
+        gather_far_bytes(0)
+        gather_far_words(1)
+        for j in range(PACK):
+            nc.scalar.copy(xb[j][:], xf[j][:])
+            gather_vector(0, j)
+        quantize(0)
+        experts(0)
+        gather_vector(1, 0)
+        gather_vector(1, 1)
+        gather_scalar(1, 2)
+        gather_scalar(1, 3)
+        gather_far_bytes(1)
+        scatter(0, 0)
+        quantize(1)
+        experts(1)
+        for nb in range(1, NB):
+            scatter(0, nb)
+        for j in range(PACK):
+            gather_scalar(2, j)
+        scatter(1, 0)
+        scatter(1, 1)
+        quantize(2)
+        experts(2)
+        scatter(1, 2)
+        scatter(1, 3)
+        for j in range(PACK):
+            gather_scalar(3, j)
+        scatter(2, 0)
+        scatter(2, 1)
+        quantize(3)
+        experts(3)
+        scatter(2, 2)
+        scatter(2, 3)
+        for h in range(2):
+            for u in range(E // 2):
+                far_expert(h * (E // 2) + u)
+            nc.sync.dma_start(out=out_rows[:, :, T + h * HALF : T + (h + 1) * HALF], in_=zs[h][:])
+        for nb in range(NB):
+            scatter(3, nb)
+            nc.sync.dma_start(out=out_rows[:, nb, 0:T], in_=win[nb][:])

@@ -31,25 +31,26 @@ def tile_moe_loc_lin_silu_kernel(
     nc = tc.nc
     with ExitStack() as ctx:
         keep = ctx.enter_context(tc.tile_pool(name="keep", bufs=1))
-        psum = ctx.enter_context(tc.psum_pool(name="psum", bufs=8))
+        psum = ctx.enter_context(tc.psum_pool(name="psum", bufs=6))
+        far_psum = ctx.enter_context(tc.psum_pool(name="far_psum", bufs=2))
 
         own_list = keep.tile([P, S // 16], U16, name="own_list")
         far_list = keep.tile([P, S // 16], U16, name="far_list")
         far_words = keep.tile([P, Q], I32, name="far_words", align_bytes=64)
         far_bytes = keep.tile([P, Q], U8, name="far_bytes", align_bytes=64)
-        xf = [keep.tile([P, T], F32, name=f"xf{j}", align_bytes=64) for j in range(PACK)]
-        xb = [keep.tile([P, T], BF16, name=f"xb{j}", align_bytes=64) for j in range(PACK)]
+        xf = [keep.tile([P, T], F32, name=f"xf{j}", align_bytes=64)[:] for j in range(PACK)]
+        xb = [keep.tile([P, T], BF16, name=f"xb{j}", tag=f"xb{j}", align_bytes=64) for j in range(PACK)]
         spans = [(0, EARLY), (EARLY, E)]
         ww = [keep.tile([P, b - a, 2 * N], U8, name=f"ww{a}", align_bytes=64) for a, b in spans]
         ws = [keep.tile([P, b - a, N], U8, name=f"ws{a}", align_bytes=64) for a, b in spans]
         gates = keep.tile([P, S], F32, name="gates", align_bytes=64)
         win = [keep.tile([P, T], F32, name=f"win{nb}", align_bytes=64) for nb in range(NB)]
 
-        nc.vector.memset(far_bytes[:].bitcast(I32), 0)
+        nc.gpsimd.memset(far_bytes[:].bitcast(I32), 0)
         for t in ws:
             nc.vector.memset(t[:].rearrange("p e n -> p (e n)").bitcast(I32), 0)
         for nb in range(NB - 1):
-            nc.vector.memset(win[nb][:], 0.0)
+            nc.gpsimd.memset(win[nb][:], 0.0)
         nc.scalar.activation(win[NB - 1][:], win[0][:], SILU)
 
         def load_weights(i):
@@ -66,15 +67,15 @@ def tile_moe_loc_lin_silu_kernel(
 
         xo_planes = xo.rearrange("(p j) t -> p j t", j=PACK)
         nc.sync.dma_start(far_list[:], offs2)
+        nc.sync.dma_start(own_list[:], offs)
         nc.sync.dma_start(out=far_words[:], in_=x_words[0].rearrange("p t d -> p (t d)").bitcast(I32))
         for r in range(4):
             nc.sync.dma_start(out=far_bytes[r:P:32, :].bitcast(I32), in_=x_scales[0, r:16:4, :].bitcast(I32))
-        nc.sync.dma_start(out=xf[0][:], in_=xo_planes[:, 0, :])
-        nc.sync.dma_start(own_list[:], offs)
-        for j in range(1, PACK):
-            nc.sync.dma_start(out=xf[j][:], in_=xo_planes[:, j, :])
+        for j in range(PACK):
+            nc.sync.dma_start(out=xf[j], in_=xo_planes[:, j, :])
         load_weights(0)
-        nc.sync.dma_start(out=gates[:], in_=gate)
+        nc.sync.dma_start(out=gates[:, : EARLY * C], in_=gate[:, : EARLY * C])
+        nc.sync.dma_start(out=gates[:, EARLY * C :], in_=gate[:, EARLY * C :])
         load_weights(1)
 
         def weights(e, nb):
@@ -92,7 +93,7 @@ def tile_moe_loc_lin_silu_kernel(
             )
 
         far_codes = [keep.tile([P, HALF], U32, name=f"far_codes{h}", align_bytes=64) for h in range(2)]
-        far_scales = [keep.tile([P, HALF], U8, name=f"far_scales{h}", align_bytes=64) for h in range(2)]
+        far_scales = {}
 
         def far_cols(h):
             return far_list[:, h * HALF // 16 : (h + 1) * HALF // 16]
@@ -101,22 +102,32 @@ def tile_moe_loc_lin_silu_kernel(
             nc.vector.tensor_copy(far_codes[h][:], far_words[:].bitcast(U32).indirect(far_cols(h)))
 
         def gather_far_bytes(h):
+            tag = "far_scales" if h == 0 else "rows0"
+            far_scales[h] = keep.tile([P, HALF], U8, name=f"far_scales{h}", tag=tag, align_bytes=64)
             nc.vector.tensor_copy(far_scales[h][:], far_bytes[:].indirect(far_cols(h)))
 
-        groups = [(0, 128), (128, 128), (256, 256), (512, 256)]
-        rows = [keep.tile([P, n, PACK], BF16, name=f"rows{s}", align_bytes=64) for s, n in groups]
-        codes = [keep.tile([P, n], U32, name=f"codes{s}", align_bytes=64) for s, n in groups]
+        groups = [(0, 128), (128, 128), (256, 128), (384, 128), (512, 256)]
+        rows = {}
+        codes = [keep.tile([P, n], U32, name=f"codes{s}", tag=f"codes{s}", align_bytes=64) for s, n in groups]
+
+        def new_rows(g):
+            s, n = groups[g]
+            tag = f"rows{s}" if g < 2 else f"codes{groups[g - 2][0]}"
+            rows[g] = keep.tile([P, n, PACK], BF16, name=f"rows{s}", tag=tag, align_bytes=64)
+
+        new_rows(0)
+        new_rows(1)
         scales = [keep.tile([P, n], U8, name=f"scales{s}", align_bytes=64) for s, n in groups]
         ys = [[keep.tile([P, n], F32, name=f"y{s}_{nb}", align_bytes=64) for nb in range(NB)] for s, n in groups[:1]]
         yw = [None] + [keep.tile([P, NB, n], F32, name=f"yw{s}", align_bytes=64) for s, n in groups[1:]]
-        zs = [keep.tile([P, NB, HALF], F32, name=f"z{h}", align_bytes=64) for h in range(2)]
+        zs = {}
 
         def own_cols(g):
             s, n = groups[g]
             return own_list[:, s // 16 : (s + n) // 16]
 
         def gather_vector(g, j):
-            nc.vector.tensor_copy(rows[g][:, :, j], xf[j][:].indirect(own_cols(g)))
+            nc.vector.tensor_copy(rows[g][:, :, j], xf[j].indirect(own_cols(g)))
 
         def gather_scalar(g, j):
             nc.scalar.activation(rows[g][:, :, j], xb[j][:].indirect(own_cols(g)), COPY)
@@ -150,7 +161,7 @@ def tile_moe_loc_lin_silu_kernel(
         def far_expert(e):
             h, u = divmod(e, E // 2)
             cols = slice(u * C, (u + 1) * C)
-            bank = psum.tile([P, NB, C], F32, name="bank")
+            bank = far_psum.tile([P, NB, C], F32, name="far_bank")
             for nb in range(NB):
                 multiply(bank[:, nb, :], e, nb, far_codes[h][:, cols], far_scales[h][:, cols])
             nc.scalar.activation(zs[h][:, :, cols], bank[:], SILU)
@@ -158,43 +169,33 @@ def tile_moe_loc_lin_silu_kernel(
         out_rows = out.rearrange("(nb p) t -> p nb t", p=P)
 
         gather_far_words(0)
-        gather_far_bytes(0)
         gather_far_words(1)
+        gather_far_bytes(0)
         for j in range(PACK):
-            nc.scalar.copy(xb[j][:], xf[j][:])
+            nc.scalar.copy(xb[j][:], xf[j])
             gather_vector(0, j)
         quantize(0)
-        experts(0)
         gather_vector(1, 0)
         gather_vector(1, 1)
         gather_scalar(1, 2)
         gather_scalar(1, 3)
         gather_far_bytes(1)
-        scatter(0, 0)
-        quantize(1)
-        experts(1)
-        for nb in range(1, NB):
-            scatter(0, nb)
-        for j in range(PACK):
-            gather_scalar(2, j)
-        scatter(1, 0)
-        scatter(1, 1)
-        quantize(2)
-        experts(2)
-        scatter(1, 2)
-        scatter(1, 3)
-        for j in range(PACK):
-            gather_scalar(3, j)
-        scatter(2, 0)
-        scatter(2, 1)
-        quantize(3)
-        experts(3)
-        scatter(2, 2)
-        scatter(2, 3)
+        last = len(groups) - 1
+        for g in range(last):
+            experts(g)
+            quantize(g + 1)
+            if g + 2 <= last:
+                new_rows(g + 2)
+                for j in range(PACK):
+                    gather_scalar(g + 2, j)
+            for nb in range(NB):
+                scatter(g, nb)
+        experts(last)
         for h in range(2):
+            zs[h] = keep.tile([P, NB, HALF], F32, name=f"z{h}", tag=f"xb{2 + h}", align_bytes=64)
             for u in range(E // 2):
                 far_expert(h * (E // 2) + u)
             nc.sync.dma_start(out=out_rows[:, :, T + h * HALF : T + (h + 1) * HALF], in_=zs[h][:])
         for nb in range(NB):
-            scatter(3, nb)
+            scatter(last, nb)
             nc.sync.dma_start(out=out_rows[:, nb, 0:T], in_=win[nb][:])

@@ -67,11 +67,12 @@ def tile_moe_loc_lin_silu_kernel(
 
         xo_planes = xo.rearrange("(p j) t -> p j t", j=PACK)
         nc.sync.dma_start(far_list[:], offs2)
-        nc.sync.dma_start(own_list[:], offs)
         nc.sync.dma_start(out=far_words[:], in_=x_words[0].rearrange("p t d -> p (t d)").bitcast(I32))
+        nc.sync.dma_start(own_list[:], offs)
+        nc.sync.dma_start(out=xf[0], in_=xo_planes[:, 0, :])
         for r in range(4):
             nc.sync.dma_start(out=far_bytes[r:P:32, :].bitcast(I32), in_=x_scales[0, r:16:4, :].bitcast(I32))
-        for j in range(PACK):
+        for j in range(1, PACK):
             nc.sync.dma_start(out=xf[j], in_=xo_planes[:, j, :])
         load_weights(0)
         nc.sync.dma_start(out=gates[:, : EARLY * C], in_=gate[:, : EARLY * C])
@@ -174,9 +175,9 @@ def tile_moe_loc_lin_silu_kernel(
         for j in range(PACK):
             nc.scalar.copy(xb[j][:], xf[j])
             gather_vector(0, j)
+            if j < 2:
+                gather_vector(1, j)
         quantize(0)
-        gather_vector(1, 0)
-        gather_vector(1, 1)
         gather_scalar(1, 2)
         gather_scalar(1, 3)
         gather_far_bytes(1)
@@ -195,7 +196,7 @@ def tile_moe_loc_lin_silu_kernel(
             zs[h] = keep.tile([P, NB, HALF], F32, name=f"z{h}", tag=f"xb{2 + h}", align_bytes=64)
             for u in range(E // 2):
                 far_expert(h * (E // 2) + u)
-            nc.sync.dma_start(out=out_rows[:, :, T + h * HALF : T + (h + 1) * HALF], in_=zs[h][:])
+            nc.scalar.dma_start(out=out_rows[:, :, T + h * HALF : T + (h + 1) * HALF], in_=zs[h][:])
         for nb in range(NB):
             scatter(last, nb)
             nc.sync.dma_start(out=out_rows[:, nb, 0:T], in_=win[nb][:])

@@ -32,7 +32,7 @@ def tile_moe_loc_lin_silu_kernel(
     with ExitStack() as ctx:
         keep = ctx.enter_context(tc.tile_pool(name="keep", bufs=1))
         psum = ctx.enter_context(tc.psum_pool(name="psum", bufs=6))
-        far_psum = ctx.enter_context(tc.psum_pool(name="far_psum", bufs=2))
+        far_psum = ctx.enter_context(tc.psum_pool(name="far_psum", bufs=1))
 
         own_list = keep.tile([P, S // 16], U16, name="own_list")
         far_list = keep.tile([P, S // 16], U16, name="far_list")
@@ -60,10 +60,11 @@ def tile_moe_loc_lin_silu_kernel(
                     out=ws[i][r:P:32, :, :].bitcast(I32),
                     in_=w_scales[a:b, 0, r:16:4, :].rearrange("e q n -> q e n").bitcast(I32),
                 )
-            nc.sync.dma_start(
-                out=ww[i][:].bitcast(I32),
-                in_=w_words[a:b, 0, :, :].rearrange("e p b -> p e b").bitcast(I32),
-            )
+            for c, d in [(a, a + 1), (a + 1, b)] if i == 0 else [(a, b)]:
+                nc.sync.dma_start(
+                    out=ww[i][:, c - a : d - a, :].bitcast(I32),
+                    in_=w_words[c:d, 0, :, :].rearrange("e p b -> p e b").bitcast(I32),
+                )
 
         xo_planes = xo.rearrange("(p j) t -> p j t", j=PACK)
         nc.sync.dma_start(far_list[:], offs2)
@@ -76,8 +77,8 @@ def tile_moe_loc_lin_silu_kernel(
             nc.sync.dma_start(out=xf[j], in_=xo_planes[:, j, :])
         load_weights(0)
         nc.sync.dma_start(out=gates[:, : EARLY * C], in_=gate[:, : EARLY * C])
-        nc.sync.dma_start(out=gates[:, EARLY * C :], in_=gate[:, EARLY * C :])
         load_weights(1)
+        nc.sync.dma_start(out=gates[:, EARLY * C :], in_=gate[:, EARLY * C :])
 
         def weights(e, nb):
             i = 0 if e < EARLY else 1
@@ -145,7 +146,10 @@ def tile_moe_loc_lin_silu_kernel(
             s, n = groups[g]
             per_bank = 1 if g == 0 else 512 // n
             for nb0 in range(0, NB, per_bank):
-                bank = psum.tile([P, per_bank, n], F32, name="bank")
+                if g == 0 and nb0 >= 2:
+                    bank = far_psum.tile([P, per_bank, n], F32, name="first_bank", tag=f"far{nb0 % 2}")
+                else:
+                    bank = psum.tile([P, per_bank, n], F32, name="bank")
                 for i in range(per_bank):
                     for u in range(n // C):
                         cols = slice(u * C, (u + 1) * C)
@@ -162,7 +166,7 @@ def tile_moe_loc_lin_silu_kernel(
         def far_expert(e):
             h, u = divmod(e, E // 2)
             cols = slice(u * C, (u + 1) * C)
-            bank = far_psum.tile([P, NB, C], F32, name="far_bank")
+            bank = far_psum.tile([P, NB, C], F32, name="far_bank", tag=f"far{e % 2}")
             for nb in range(NB):
                 multiply(bank[:, nb, :], e, nb, far_codes[h][:, cols], far_scales[h][:, cols])
             nc.scalar.activation(zs[h][:, :, cols], bank[:], SILU)

@@ -21,8 +21,8 @@ MULT = mybir.AluOpType.mult
 P = 128
 PACK = 4
 NB = N // P
-HALF = S // 2
 EARLY = 2
+PAIR = 2 * C
 
 
 def tile_moe_loc_lin_silu_kernel(
@@ -31,15 +31,13 @@ def tile_moe_loc_lin_silu_kernel(
     nc = tc.nc
     with ExitStack() as ctx:
         keep = ctx.enter_context(tc.tile_pool(name="keep", bufs=1))
-        psum = ctx.enter_context(tc.psum_pool(name="psum", bufs=6))
-        far_psum = ctx.enter_context(tc.psum_pool(name="far_psum", bufs=1))
+        psum = ctx.enter_context(tc.psum_pool(name="psum", bufs=1))
 
         own_list = keep.tile([P, S // 16], U16, name="own_list")
         far_list = keep.tile([P, S // 16], U16, name="far_list")
         far_words = keep.tile([P, Q], I32, name="far_words", align_bytes=64)
         far_bytes = keep.tile([P, Q], U8, name="far_bytes", align_bytes=64)
         xf = [keep.tile([P, T], F32, name=f"xf{j}", align_bytes=64)[:] for j in range(PACK)]
-        xb = [keep.tile([P, T], BF16, name=f"xb{j}", tag=f"xb{j}", align_bytes=64) for j in range(PACK)]
         spans = [(0, EARLY), (EARLY, E)]
         ww = [keep.tile([P, b - a, 2 * N], U8, name=f"ww{a}", align_bytes=64) for a, b in spans]
         ws = [keep.tile([P, b - a, N], U8, name=f"ws{a}", align_bytes=64) for a, b in spans]
@@ -67,14 +65,22 @@ def tile_moe_loc_lin_silu_kernel(
                 )
 
         xo_planes = xo.rearrange("(p j) t -> p j t", j=PACK)
+
+        def load_plane(j):
+            nc.sync.dma_start(out=xf[j], in_=xo_planes[:, j, :])
+
+        def load_far_bytes(queue):
+            for r in range(4):
+                queue.dma_start(out=far_bytes[r:P:32, :].bitcast(I32), in_=x_scales[0, r:16:4, :].bitcast(I32))
+
         nc.sync.dma_start(far_list[:], offs2)
         nc.sync.dma_start(out=far_words[:], in_=x_words[0].rearrange("p t d -> p (t d)").bitcast(I32))
         nc.sync.dma_start(own_list[:], offs)
-        nc.sync.dma_start(out=xf[0], in_=xo_planes[:, 0, :])
-        for r in range(4):
-            nc.sync.dma_start(out=far_bytes[r:P:32, :].bitcast(I32), in_=x_scales[0, r:16:4, :].bitcast(I32))
-        for j in range(1, PACK):
-            nc.sync.dma_start(out=xf[j], in_=xo_planes[:, j, :])
+        load_plane(0)
+        load_plane(1)
+        load_far_bytes(nc.sync)
+        load_plane(2)
+        load_plane(3)
         load_weights(0)
         nc.sync.dma_start(out=gates[:, : EARLY * C], in_=gate[:, : EARLY * C])
         load_weights(1)
@@ -94,35 +100,36 @@ def tile_moe_loc_lin_silu_kernel(
                 out=dst, lhsT=w, lhsT_scale=s, rhs=codes.bitcast(FP8X4), rhs_scale=scales, start=True, stop=True
             )
 
-        far_codes = [keep.tile([P, HALF], U32, name=f"far_codes{h}", align_bytes=64) for h in range(2)]
-        far_scales = {}
+        far_codes, far_scales = {}, {}
 
-        def far_cols(h):
-            return far_list[:, h * HALF // 16 : (h + 1) * HALF // 16]
+        def far_cols(a, b):
+            return far_list[:, a * C // 16 : b * C // 16]
 
-        def gather_far_words(h):
-            nc.vector.tensor_copy(far_codes[h][:], far_words[:].bitcast(U32).indirect(far_cols(h)))
+        def gather_far_words(a, b):
+            t = keep.tile([P, (b - a) * C], U32, name=f"far_codes{a}", align_bytes=64)
+            nc.vector.tensor_copy(t[:], far_words[:].bitcast(U32).indirect(far_cols(a, b)))
+            for e in range(a, b):
+                far_codes[e] = t[:, (e - a) * C : (e - a + 1) * C]
 
-        def gather_far_bytes(h):
-            tag = "far_scales" if h == 0 else "rows0"
-            far_scales[h] = keep.tile([P, HALF], U8, name=f"far_scales{h}", tag=tag, align_bytes=64)
-            nc.vector.tensor_copy(far_scales[h][:], far_bytes[:].indirect(far_cols(h)))
+        def gather_far_bytes(a, b, tag):
+            t = keep.tile([P, (b - a) * C], U8, name=f"far_scales{a}", tag=tag, align_bytes=64)
+            nc.vector.tensor_copy(t[:], far_bytes[:].indirect(far_cols(a, b)))
+            for e in range(a, b):
+                far_scales[e] = t[:, (e - a) * C : (e - a + 1) * C]
 
         groups = [(0, 128), (128, 128), (256, 128), (384, 128), (512, 256)]
-        rows = {}
+        rows, xb, banks, zs = {}, {}, {}, {}
         codes = [keep.tile([P, n], U32, name=f"codes{s}", tag=f"codes{s}", align_bytes=64) for s, n in groups]
+        scales = [keep.tile([P, n], U8, name=f"scales{s}", tag=f"scales{s}", align_bytes=64) for s, n in groups]
+        yw = {}
 
-        def new_rows(g):
+        def new_rows(g, tag):
             s, n = groups[g]
-            tag = f"rows{s}" if g < 2 else f"codes{groups[g - 2][0]}"
             rows[g] = keep.tile([P, n, PACK], BF16, name=f"rows{s}", tag=tag, align_bytes=64)
 
-        new_rows(0)
-        new_rows(1)
-        scales = [keep.tile([P, n], U8, name=f"scales{s}", align_bytes=64) for s, n in groups]
-        ys = [[keep.tile([P, n], F32, name=f"y{s}_{nb}", align_bytes=64) for nb in range(NB)] for s, n in groups[:1]]
-        yw = [None] + [keep.tile([P, NB, n], F32, name=f"yw{s}", align_bytes=64) for s, n in groups[1:]]
-        zs = {}
+        def cast(j, tag):
+            xb[j] = keep.tile([P, T], BF16, name=f"xb{j}", tag=tag, align_bytes=64)
+            nc.scalar.copy(xb[j][:], xf[j])
 
         def own_cols(g):
             s, n = groups[g]
@@ -139,68 +146,98 @@ def tile_moe_loc_lin_silu_kernel(
                 out=codes[g][:].bitcast(FP8X4), scales=scales[g][:], in_=rows[g][:].rearrange("p n j -> p (n j)")
             )
 
-        def result(g, nb):
-            return ys[0][nb][:] if g == 0 else yw[g][:, nb, :]
-
-        def experts(g):
+        def products(g, lo, hi, tag):
             s, n = groups[g]
-            per_bank = 1 if g == 0 else 512 // n
-            for nb0 in range(0, NB, per_bank):
-                if g == 0 and nb0 >= 2:
-                    bank = far_psum.tile([P, per_bank, n], F32, name="first_bank", tag=f"far{nb0 % 2}")
-                else:
-                    bank = psum.tile([P, per_bank, n], F32, name="bank")
-                for i in range(per_bank):
-                    for u in range(n // C):
-                        cols = slice(u * C, (u + 1) * C)
-                        multiply(bank[:, i, cols], s // C + u, nb0 + i, codes[g][:, cols], scales[g][:, cols])
-                if g == 0:
-                    nc.scalar.activation(ys[0][nb0][:], bank[:, 0, :], SILU)
-                else:
-                    nc.scalar.activation(yw[g][:, nb0 : nb0 + per_bank, :], bank[:], SILU)
+            bank = psum.tile([P, hi - lo, n], F32, name=f"bank{g}_{lo}", tag=tag)
+            for nb in range(lo, hi):
+                banks[g, nb] = (bank, lo)
+                for u in range(n // C):
+                    cols = slice(u * C, (u + 1) * C)
+                    multiply(bank[:, nb - lo, cols], s // C + u, nb, codes[g][:, cols], scales[g][:, cols])
 
-        def scatter(g, nb):
+        def silu(g, lo, hi):
             s, n = groups[g]
-            nc.vector.tensor_tensor(win[nb][:].indirect(own_cols(g)), result(g, nb), gates[:, s : s + n], MULT)
+            bank, first = banks[g, lo]
+            y = keep.tile([P, hi - lo, n], F32, name=f"y{g}_{lo}", align_bytes=64)
+            nc.scalar.activation(y[:], bank[:, lo - first : hi - first, :], SILU)
+            for nb in range(lo, hi):
+                yw[g, nb] = y[:, nb - lo, :]
 
-        def far_expert(e):
-            h, u = divmod(e, E // 2)
-            cols = slice(u * C, (u + 1) * C)
-            bank = far_psum.tile([P, NB, C], F32, name="far_bank", tag=f"far{e % 2}")
-            for nb in range(NB):
-                multiply(bank[:, nb, :], e, nb, far_codes[h][:, cols], far_scales[h][:, cols])
-            nc.scalar.activation(zs[h][:, :, cols], bank[:], SILU)
+        def scatter(g, lo, hi):
+            s, n = groups[g]
+            for nb in range(lo, hi):
+                nc.vector.tensor_tensor(win[nb][:].indirect(own_cols(g)), yw[g, nb], gates[:, s : s + n], MULT)
 
         out_rows = out.rearrange("(nb p) t -> p nb t", p=P)
 
-        gather_far_words(0)
-        gather_far_words(1)
-        gather_far_bytes(0)
-        for j in range(PACK):
-            nc.scalar.copy(xb[j][:], xf[j])
-            gather_vector(0, j)
-            if j < 2:
-                gather_vector(1, j)
-        quantize(0)
-        gather_scalar(1, 2)
-        gather_scalar(1, 3)
-        gather_far_bytes(1)
-        last = len(groups) - 1
-        for g in range(last):
-            experts(g)
-            quantize(g + 1)
-            if g + 2 <= last:
-                new_rows(g + 2)
-                for j in range(PACK):
-                    gather_scalar(g + 2, j)
+        def far_expert(e):
+            bank = psum.tile([P, NB, C], F32, name=f"far_bank{e}", tag=f"b{e % 3}")
             for nb in range(NB):
-                scatter(g, nb)
-        experts(last)
-        for h in range(2):
-            zs[h] = keep.tile([P, NB, HALF], F32, name=f"z{h}", tag=f"xb{2 + h}", align_bytes=64)
-            for u in range(E // 2):
-                far_expert(h * (E // 2) + u)
-            nc.scalar.dma_start(out=out_rows[:, :, T + h * HALF : T + (h + 1) * HALF], in_=zs[h][:])
+                multiply(bank[:, nb, :], e, nb, far_codes[e], far_scales[e])
+            i, v = divmod(e, 2)
+            if v == 0:
+                zs[i] = keep.tile([P, NB, PAIR], F32, name=f"z{i}", tag=f"xb{i}", align_bytes=64)
+            nc.scalar.activation(zs[i][:, :, v * C : (v + 1) * C], bank[:], SILU)
+            if v == 1:
+                nc.scalar.dma_start(out=out_rows[:, :, T + i * PAIR : T + (i + 1) * PAIR], in_=zs[i][:])
+
+        gather_far_words(0, 4)
+        gather_far_words(4, E)
+        gather_far_bytes(0, 4, "far_scales0")
+        new_rows(0, "rows0")
+        new_rows(1, "rows1")
+        for j in range(3):
+            cast(j, f"xb{j}")
+            gather_vector(0, j)
+        gather_scalar(1, 0)
+        gather_scalar(1, 1)
+        gather_vector(1, 2)
+        gather_vector(0, 3)
+        quantize(0)
+        gather_vector(1, 3)
+        gather_far_bytes(4, E, "rows0")
+        quantize(1)
+        products(0, 0, 1, "b0")
+        silu(0, 0, 1)
+        products(0, 1, 4, "b1")
+        silu(0, 1, 4)
+        products(1, 0, 4, "b2")
+        silu(1, 0, 2)
+        scatter(0, 0, 4)
+        scatter(1, 0, 2)
+        cast(3, "codes0")
+        new_rows(2, "scales0")
+        for j in range(PACK):
+            gather_scalar(2, j)
+        quantize(2)
+        products(2, 0, 4, "b3")
+        silu(1, 2, 4)
+        scatter(1, 2, 4)
+        new_rows(3, "codes128")
+        for j in range(PACK):
+            gather_scalar(3, j)
+        quantize(3)
+        products(3, 0, 4, "b4")
+        silu(2, 0, 4)
+        scatter(2, 0, 4)
+        new_rows(4, "codes256")
+        gather_scalar(4, 0)
+        gather_scalar(4, 1)
+        silu(3, 0, 2)
+        scatter(3, 0, 2)
+        gather_scalar(4, 2)
+        gather_scalar(4, 3)
+        quantize(4)
+        products(4, 0, 2, "b5")
+        products(4, 2, 4, "b6")
+        silu(3, 2, 4)
+        scatter(3, 2, 4)
+        for e in range(3):
+            far_expert(e)
+        silu(4, 0, 2)
+        silu(4, 2, 4)
+        for e in range(3, E):
+            far_expert(e)
         for nb in range(NB):
-            scatter(last, nb)
+            scatter(4, nb, nb + 1)
             nc.sync.dma_start(out=out_rows[:, nb, 0:T], in_=win[nb][:])

@@ -73,8 +73,8 @@ def tile_moe_loc_lin_silu_kernel(
             for r in range(4):
                 queue.dma_start(out=far_bytes[r:P:32, :].bitcast(I32), in_=x_scales[0, r:16:4, :].bitcast(I32))
 
-        nc.sync.dma_start(far_list[:], offs2)
         nc.sync.dma_start(out=far_words[:], in_=x_words[0].rearrange("p t d -> p (t d)").bitcast(I32))
+        nc.sync.dma_start(far_list[:], offs2)
         nc.sync.dma_start(own_list[:], offs)
         load_plane(0)
         load_plane(1)
@@ -171,7 +171,7 @@ def tile_moe_loc_lin_silu_kernel(
         out_rows = out.rearrange("(nb p) t -> p nb t", p=P)
 
         def far_expert(e):
-            bank = psum.tile([P, NB, C], F32, name=f"far_bank{e}", tag=f"b{e % 3}")
+            bank = psum.tile([P, NB, C], F32, name=f"far_bank{e}", tag=f"b{(0, 1, 2, 7, 3, 4)[e]}")
             for nb in range(NB):
                 multiply(bank[:, nb, :], e, nb, far_codes[e], far_scales[e])
             i, v = divmod(e, 2)
@@ -235,9 +235,9 @@ def tile_moe_loc_lin_silu_kernel(
         for e in range(3):
             far_expert(e)
         silu(4, 0, 2)
-        silu(4, 2, 4)
         for e in range(3, E):
             far_expert(e)
+        silu(4, 2, 4)
         for nb in range(NB):
             scatter(4, nb, nb + 1)
             nc.sync.dma_start(out=out_rows[:, nb, 0:T], in_=win[nb][:])

@@ -21,8 +21,14 @@ MULT = mybir.AluOpType.mult
 P = 128
 PACK = 4
 NB = N // P
+ENTRIES = 16
+QUAD = 32
+SCALE_ROWS = K // 32
 EARLY = 2
 PAIR = 2 * C
+FAR_CUT = 4
+GROUPS = [(0, C), (C, C), (2 * C, C), (3 * C, C), (4 * C, 2 * C)]
+FAR_BANKS = (0, 1, 2, 7, 3, 4)
 
 
 def tile_moe_loc_lin_silu_kernel(
@@ -33,122 +39,130 @@ def tile_moe_loc_lin_silu_kernel(
         keep = ctx.enter_context(tc.tile_pool(name="keep", bufs=1))
         psum = ctx.enter_context(tc.psum_pool(name="psum", bufs=1))
 
-        own_list = keep.tile([P, S // 16], U16, name="own_list")
-        far_list = keep.tile([P, S // 16], U16, name="far_list")
+        own_list = keep.tile([P, S // ENTRIES], U16, name="own_list")
+        far_list = keep.tile([P, S // ENTRIES], U16, name="far_list")
         far_words = keep.tile([P, Q], I32, name="far_words", align_bytes=64)
         far_bytes = keep.tile([P, Q], U8, name="far_bytes", align_bytes=64)
-        xf = [keep.tile([P, T], F32, name=f"xf{j}", align_bytes=64)[:] for j in range(PACK)]
+        planes = [keep.tile([P, T], F32, name=f"plane{j}", align_bytes=64) for j in range(PACK)]
         spans = [(0, EARLY), (EARLY, E)]
-        ww = [keep.tile([P, b - a, 2 * N], U8, name=f"ww{a}", align_bytes=64) for a, b in spans]
-        ws = [keep.tile([P, b - a, N], U8, name=f"ws{a}", align_bytes=64) for a, b in spans]
+        w_codes = [keep.tile([P, b - a, 2 * N], U8, name=f"w_codes{a}", align_bytes=64) for a, b in spans]
+        w_bytes = [keep.tile([P, b - a, N], U8, name=f"w_bytes{a}", align_bytes=64) for a, b in spans]
         gates = keep.tile([P, S], F32, name="gates", align_bytes=64)
-        win = [keep.tile([P, T], F32, name=f"win{nb}", align_bytes=64) for nb in range(NB)]
+        windows = [keep.tile([P, T], F32, name=f"window{nb}", align_bytes=64) for nb in range(NB)]
 
         nc.gpsimd.memset(far_bytes[:].bitcast(I32), 0)
-        for t in ws:
-            nc.vector.memset(t[:].rearrange("p e n -> p (e n)").bitcast(I32), 0)
+        for tile in w_bytes:
+            nc.vector.memset(tile[:].rearrange("p e n -> p (e n)").bitcast(I32), 0)
         for nb in range(NB - 1):
-            nc.gpsimd.memset(win[nb][:], 0.0)
-        nc.scalar.activation(win[NB - 1][:], win[0][:], SILU)
+            nc.gpsimd.memset(windows[nb][:], 0.0)
+        nc.scalar.activation(windows[NB - 1][:], windows[0][:], SILU)
+
+        xo_planes = xo.rearrange("(p j) t -> p j t", j=PACK)
+
+        def load_plane(j):
+            nc.sync.dma_start(out=planes[j][:], in_=xo_planes[:, j, :])
 
         def load_weights(i):
             a, b = spans[i]
             for r in range(4):
                 nc.sync.dma_start(
-                    out=ws[i][r:P:32, :, :].bitcast(I32),
-                    in_=w_scales[a:b, 0, r:16:4, :].rearrange("e q n -> q e n").bitcast(I32),
+                    out=w_bytes[i][r:P:QUAD, :, :].bitcast(I32),
+                    in_=w_scales[a:b, 0, r:SCALE_ROWS:4, :].rearrange("e q n -> q e n").bitcast(I32),
                 )
             for c, d in [(a, a + 1), (a + 1, b)] if i == 0 else [(a, b)]:
                 nc.sync.dma_start(
-                    out=ww[i][:, c - a : d - a, :].bitcast(I32),
+                    out=w_codes[i][:, c - a : d - a, :].bitcast(I32),
                     in_=w_words[c:d, 0, :, :].rearrange("e p b -> p e b").bitcast(I32),
                 )
-
-        xo_planes = xo.rearrange("(p j) t -> p j t", j=PACK)
-
-        def load_plane(j):
-            nc.sync.dma_start(out=xf[j], in_=xo_planes[:, j, :])
-
-        def load_far_bytes(queue):
-            for r in range(4):
-                queue.dma_start(out=far_bytes[r:P:32, :].bitcast(I32), in_=x_scales[0, r:16:4, :].bitcast(I32))
+            nc.sync.dma_start(out=gates[:, a * C : b * C], in_=gate[:, a * C : b * C])
 
         nc.sync.dma_start(out=far_words[:], in_=x_words[0].rearrange("p t d -> p (t d)").bitcast(I32))
         nc.sync.dma_start(far_list[:], offs2)
         nc.sync.dma_start(own_list[:], offs)
         load_plane(0)
         load_plane(1)
-        load_far_bytes(nc.sync)
+        for r in range(4):
+            nc.sync.dma_start(
+                out=far_bytes[r:P:QUAD, :].bitcast(I32), in_=x_scales[0, r:SCALE_ROWS:4, :].bitcast(I32)
+            )
         load_plane(2)
         load_plane(3)
         load_weights(0)
-        nc.sync.dma_start(out=gates[:, : EARLY * C], in_=gate[:, : EARLY * C])
         load_weights(1)
-        nc.sync.dma_start(out=gates[:, EARLY * C :], in_=gate[:, EARLY * C :])
 
-        def weights(e, nb):
+        def multiply(dst, e, nb, token_codes, token_scales):
             i = 0 if e < EARLY else 1
-            le = e - spans[i][0]
-            return (
-                ww[i][:, le, 2 * P * nb : 2 * P * (nb + 1)].bitcast(FP4X4),
-                ws[i][:, le, P * nb : P * (nb + 1)],
-            )
-
-        def multiply(dst, e, nb, codes, scales):
-            w, s = weights(e, nb)
+            local = e - spans[i][0]
             nc.tensor.matmul_mx(
-                out=dst, lhsT=w, lhsT_scale=s, rhs=codes.bitcast(FP8X4), rhs_scale=scales, start=True, stop=True
+                out=dst,
+                lhsT=w_codes[i][:, local, 2 * P * nb : 2 * P * (nb + 1)].bitcast(FP4X4),
+                lhsT_scale=w_bytes[i][:, local, P * nb : P * (nb + 1)],
+                rhs=token_codes.bitcast(FP8X4),
+                rhs_scale=token_scales,
+                start=True,
+                stop=True,
             )
 
-        far_codes, far_scales = {}, {}
+        far_codes, far_scales, far_out = {}, {}, {}
+        out_rows = out.rearrange("(nb p) t -> p nb t", p=P)
 
-        def far_cols(a, b):
-            return far_list[:, a * C // 16 : b * C // 16]
+        def far_entries(a, b):
+            return far_list[:, a * C // ENTRIES : b * C // ENTRIES]
 
         def gather_far_words(a, b):
-            t = keep.tile([P, (b - a) * C], U32, name=f"far_codes{a}", align_bytes=64)
-            nc.vector.tensor_copy(t[:], far_words[:].bitcast(U32).indirect(far_cols(a, b)))
+            tile = keep.tile([P, (b - a) * C], U32, name=f"far_codes{a}", align_bytes=64)
+            nc.vector.tensor_copy(tile[:], far_words[:].bitcast(U32).indirect(far_entries(a, b)))
             for e in range(a, b):
-                far_codes[e] = t[:, (e - a) * C : (e - a + 1) * C]
+                far_codes[e] = tile[:, (e - a) * C : (e - a + 1) * C]
 
         def gather_far_bytes(a, b, tag):
-            t = keep.tile([P, (b - a) * C], U8, name=f"far_scales{a}", tag=tag, align_bytes=64)
-            nc.vector.tensor_copy(t[:], far_bytes[:].indirect(far_cols(a, b)))
+            tile = keep.tile([P, (b - a) * C], U8, name=f"far_scales{a}", tag=tag, align_bytes=64)
+            nc.vector.tensor_copy(tile[:], far_bytes[:].indirect(far_entries(a, b)))
             for e in range(a, b):
-                far_scales[e] = t[:, (e - a) * C : (e - a + 1) * C]
+                far_scales[e] = tile[:, (e - a) * C : (e - a + 1) * C]
 
-        groups = [(0, 128), (128, 128), (256, 128), (384, 128), (512, 256)]
-        rows, xb, banks, zs = {}, {}, {}, {}
-        codes = [keep.tile([P, n], U32, name=f"codes{s}", tag=f"codes{s}", align_bytes=64) for s, n in groups]
-        scales = [keep.tile([P, n], U8, name=f"scales{s}", tag=f"scales{s}", align_bytes=64) for s, n in groups]
-        yw = {}
+        def far_expert(e):
+            bank = psum.tile([P, NB, C], F32, name=f"far_bank{e}", tag=f"bank{FAR_BANKS[e]}")
+            for nb in range(NB):
+                multiply(bank[:, nb, :], e, nb, far_codes[e], far_scales[e])
+            i, second = divmod(e, 2)
+            if not second:
+                far_out[i] = keep.tile([P, NB, PAIR], F32, name=f"far_out{i}", tag=f"cast{i}", align_bytes=64)
+            nc.scalar.activation(far_out[i][:, :, second * C : (second + 1) * C], bank[:], SILU)
+            if second:
+                nc.scalar.dma_start(out=out_rows[:, :, T + i * PAIR : T + (i + 1) * PAIR], in_=far_out[i][:])
+
+        rows, casts, banks, results = {}, {}, {}, {}
+        codes = [keep.tile([P, n], U32, name=f"codes{s}", tag=f"codes{s}", align_bytes=64) for s, n in GROUPS]
+        scales = [keep.tile([P, n], U8, name=f"scales{s}", tag=f"scales{s}", align_bytes=64) for s, n in GROUPS]
+
+        def own_entries(g):
+            s, n = GROUPS[g]
+            return own_list[:, s // ENTRIES : (s + n) // ENTRIES]
 
         def new_rows(g, tag):
-            s, n = groups[g]
+            s, n = GROUPS[g]
             rows[g] = keep.tile([P, n, PACK], BF16, name=f"rows{s}", tag=tag, align_bytes=64)
 
         def cast(j, tag):
-            xb[j] = keep.tile([P, T], BF16, name=f"xb{j}", tag=tag, align_bytes=64)
-            nc.scalar.copy(xb[j][:], xf[j])
-
-        def own_cols(g):
-            s, n = groups[g]
-            return own_list[:, s // 16 : (s + n) // 16]
+            casts[j] = keep.tile([P, T], BF16, name=f"cast{j}", tag=tag, align_bytes=64)
+            nc.scalar.copy(casts[j][:], planes[j][:])
 
         def gather_vector(g, j):
-            nc.vector.tensor_copy(rows[g][:, :, j], xf[j].indirect(own_cols(g)))
+            nc.vector.tensor_copy(rows[g][:, :, j], planes[j][:].indirect(own_entries(g)))
 
-        def gather_scalar(g, j):
-            nc.scalar.activation(rows[g][:, :, j], xb[j][:].indirect(own_cols(g)), COPY)
+        def gather_scalar(g, lo, hi):
+            for j in range(lo, hi):
+                nc.scalar.activation(rows[g][:, :, j], casts[j][:].indirect(own_entries(g)), COPY)
 
         def quantize(g):
             nc.vector.quantize_mx(
                 out=codes[g][:].bitcast(FP8X4), scales=scales[g][:], in_=rows[g][:].rearrange("p n j -> p (n j)")
             )
 
-        def products(g, lo, hi, tag):
-            s, n = groups[g]
-            bank = psum.tile([P, hi - lo, n], F32, name=f"bank{g}_{lo}", tag=tag)
+        def products(g, lo, hi, b):
+            s, n = GROUPS[g]
+            bank = psum.tile([P, hi - lo, n], F32, name=f"bank{g}_{lo}", tag=f"bank{b}")
             for nb in range(lo, hi):
                 banks[g, nb] = (bank, lo)
                 for u in range(n // C):
@@ -156,88 +170,82 @@ def tile_moe_loc_lin_silu_kernel(
                     multiply(bank[:, nb - lo, cols], s // C + u, nb, codes[g][:, cols], scales[g][:, cols])
 
         def silu(g, lo, hi):
-            s, n = groups[g]
+            n = GROUPS[g][1]
             bank, first = banks[g, lo]
-            y = keep.tile([P, hi - lo, n], F32, name=f"y{g}_{lo}", align_bytes=64)
-            nc.scalar.activation(y[:], bank[:, lo - first : hi - first, :], SILU)
+            tile = keep.tile([P, hi - lo, n], F32, name=f"result{g}_{lo}", align_bytes=64)
+            nc.scalar.activation(tile[:], bank[:, lo - first : hi - first, :], SILU)
             for nb in range(lo, hi):
-                yw[g, nb] = y[:, nb - lo, :]
+                results[g, nb] = tile[:, nb - lo, :]
 
         def scatter(g, lo, hi):
-            s, n = groups[g]
+            s, n = GROUPS[g]
             for nb in range(lo, hi):
-                nc.vector.tensor_tensor(win[nb][:].indirect(own_cols(g)), yw[g, nb], gates[:, s : s + n], MULT)
+                nc.vector.tensor_tensor(
+                    windows[nb][:].indirect(own_entries(g)), results[g, nb], gates[:, s : s + n], MULT
+                )
 
-        out_rows = out.rearrange("(nb p) t -> p nb t", p=P)
-
-        def far_expert(e):
-            bank = psum.tile([P, NB, C], F32, name=f"far_bank{e}", tag=f"b{(0, 1, 2, 7, 3, 4)[e]}")
-            for nb in range(NB):
-                multiply(bank[:, nb, :], e, nb, far_codes[e], far_scales[e])
-            i, v = divmod(e, 2)
-            if v == 0:
-                zs[i] = keep.tile([P, NB, PAIR], F32, name=f"z{i}", tag=f"xb{i}", align_bytes=64)
-            nc.scalar.activation(zs[i][:, :, v * C : (v + 1) * C], bank[:], SILU)
-            if v == 1:
-                nc.scalar.dma_start(out=out_rows[:, :, T + i * PAIR : T + (i + 1) * PAIR], in_=zs[i][:])
-
-        gather_far_words(0, 4)
-        gather_far_words(4, E)
-        gather_far_bytes(0, 4, "far_scales0")
+        gather_far_words(0, FAR_CUT)
+        gather_far_words(FAR_CUT, E)
+        gather_far_bytes(0, FAR_CUT, "far_scales0")
         new_rows(0, "rows0")
         new_rows(1, "rows1")
-        for j in range(3):
-            cast(j, f"xb{j}")
+        for j in range(PACK - 1):
+            cast(j, f"cast{j}")
             gather_vector(0, j)
-        gather_scalar(1, 0)
-        gather_scalar(1, 1)
+        gather_scalar(1, 0, 2)
         gather_vector(1, 2)
         gather_vector(0, 3)
         quantize(0)
         gather_vector(1, 3)
-        gather_far_bytes(4, E, "rows0")
+        gather_far_bytes(FAR_CUT, E, "rows0")
         quantize(1)
-        products(0, 0, 1, "b0")
+
+        products(0, 0, 1, 0)
         silu(0, 0, 1)
-        products(0, 1, 4, "b1")
-        silu(0, 1, 4)
-        products(1, 0, 4, "b2")
+        products(0, 1, NB, 1)
+        silu(0, 1, NB)
+        products(1, 0, NB, 2)
         silu(1, 0, 2)
-        scatter(0, 0, 4)
+        scatter(0, 0, NB)
         scatter(1, 0, 2)
-        cast(3, "codes0")
+
+        cast(PACK - 1, "codes0")
         new_rows(2, "scales0")
-        for j in range(PACK):
-            gather_scalar(2, j)
+        gather_scalar(2, 0, PACK)
         quantize(2)
-        products(2, 0, 4, "b3")
-        silu(1, 2, 4)
-        scatter(1, 2, 4)
-        new_rows(3, "codes128")
-        for j in range(PACK):
-            gather_scalar(3, j)
+        products(2, 0, NB, 3)
+        silu(1, 2, NB)
+        scatter(1, 2, NB)
+
+        new_rows(3, f"codes{GROUPS[1][0]}")
+        gather_scalar(3, 0, PACK - 1)
+        silu(2, 0, 1)
+        scatter(2, 0, 1)
+        gather_scalar(3, PACK - 1, PACK)
         quantize(3)
-        products(3, 0, 4, "b4")
-        silu(2, 0, 4)
-        scatter(2, 0, 4)
-        new_rows(4, "codes256")
-        gather_scalar(4, 0)
-        gather_scalar(4, 1)
+        products(3, 0, NB, 4)
+        silu(2, 1, NB)
+        scatter(2, 1, NB)
+
+        new_rows(4, f"codes{GROUPS[2][0]}")
+        gather_scalar(4, 0, 2)
         silu(3, 0, 2)
         scatter(3, 0, 2)
-        gather_scalar(4, 2)
-        gather_scalar(4, 3)
+        gather_scalar(4, 2, PACK)
         quantize(4)
-        products(4, 0, 2, "b5")
-        products(4, 2, 4, "b6")
-        silu(3, 2, 4)
-        scatter(3, 2, 4)
+        products(4, 0, 2, 5)
+        products(4, 2, NB, 6)
+        silu(3, 2, NB)
+        scatter(3, 2, NB)
+
         for e in range(3):
             far_expert(e)
-        silu(4, 0, 2)
-        for e in range(3, E):
-            far_expert(e)
-        silu(4, 2, 4)
+        silu(4, 0, 1)
+        far_expert(3)
+        far_expert(4)
+        silu(4, 1, 2)
+        far_expert(5)
+        silu(4, 2, NB)
         for nb in range(NB):
             scatter(4, nb, nb + 1)
-            nc.sync.dma_start(out=out_rows[:, nb, 0:T], in_=win[nb][:])
+            nc.sync.dma_start(out=out_rows[:, nb, 0:T], in_=windows[nb][:])

@@ -205,17 +205,17 @@ def tile_moe_loc_lin_silu_kernel(
         products(0, 1, NB, 1)
         silu(0, 1, NB)
         products(1, 0, NB, 2)
-        silu(1, 0, 2)
+        silu(1, 0, 1)
         scatter(0, 0, NB)
-        scatter(1, 0, 2)
+        scatter(1, 0, 1)
 
         cast(PACK - 1, "codes0")
         new_rows(2, "scales0")
         gather_scalar(2, 0, PACK)
         quantize(2)
         products(2, 0, NB, 3)
-        silu(1, 2, NB)
-        scatter(1, 2, NB)
+        silu(1, 1, NB)
+        scatter(1, 1, NB)
 
         new_rows(3, f"codes{GROUPS[1][0]}")
         gather_scalar(3, 0, PACK - 1)
@@ -229,14 +229,14 @@ def tile_moe_loc_lin_silu_kernel(
 
         new_rows(4, f"codes{GROUPS[2][0]}")
         gather_scalar(4, 0, 2)
-        silu(3, 0, 2)
-        scatter(3, 0, 2)
+        silu(3, 0, 1)
+        scatter(3, 0, 1)
         gather_scalar(4, 2, PACK)
         quantize(4)
         products(4, 0, 2, 5)
         products(4, 2, NB, 6)
-        silu(3, 2, NB)
-        scatter(3, 2, NB)
+        silu(3, 1, NB)
+        scatter(3, 1, NB)
 
         for e in range(3):
             far_expert(e)

@@ -248,4 +248,8 @@ def tile_moe_loc_lin_silu_kernel(
         silu(4, 2, NB)
         for nb in range(NB):
             scatter(4, nb, nb + 1)
-            nc.sync.dma_start(out=out_rows[:, nb, 0:T], in_=windows[nb][:])
+            if nb < NB - 1:
+                nc.sync.dma_start(out=out_rows[:, nb, 0:T], in_=windows[nb][:])
+            else:
+                nc.sync.dma_start(out=out_rows[:, nb, 0 : T // 2], in_=windows[nb][:, 0 : T // 2])
+                nc.scalar.dma_start(out=out_rows[:, nb, T // 2 : T], in_=windows[nb][:, T // 2 : T])

@@ -26,9 +26,7 @@ QUAD = 32
 SCALE_ROWS = K // 32
 EARLY = 2
 PAIR = 2 * C
-FAR_CUT = 4
-GROUPS = [(0, C), (C, C), (2 * C, C), (3 * C, C), (4 * C, 2 * C)]
-FAR_BANKS = (0, 1, 2, 7, 3, 4)
+GROUPS = S // PAIR
 
 
 def tile_moe_loc_lin_silu_kernel(
@@ -46,13 +44,12 @@ def tile_moe_loc_lin_silu_kernel(
         planes = [keep.tile([P, T], F32, name=f"plane{j}", align_bytes=64) for j in range(PACK)]
         spans = [(0, EARLY), (EARLY, E)]
         w_codes = [keep.tile([P, b - a, 2 * N], U8, name=f"w_codes{a}", align_bytes=64) for a, b in spans]
-        w_bytes = [keep.tile([P, b - a, N], U8, name=f"w_bytes{a}", align_bytes=64) for a, b in spans]
+        w_bytes = keep.tile([P, E, N], U8, name="w_bytes", align_bytes=64)
         gates = keep.tile([P, S], F32, name="gates", align_bytes=64)
         windows = [keep.tile([P, T], F32, name=f"window{nb}", align_bytes=64) for nb in range(NB)]
 
         nc.gpsimd.memset(far_bytes[:].bitcast(I32), 0)
-        for tile in w_bytes:
-            nc.vector.memset(tile[:].rearrange("p e n -> p (e n)").bitcast(I32), 0)
+        nc.vector.memset(w_bytes[:].rearrange("p e n -> p (e n)").bitcast(I32), 0)
         for nb in range(NB - 1):
             nc.gpsimd.memset(windows[nb][:], 0.0)
         nc.scalar.activation(windows[NB - 1][:], windows[0][:], SILU)
@@ -62,19 +59,16 @@ def tile_moe_loc_lin_silu_kernel(
         def load_plane(j):
             nc.sync.dma_start(out=planes[j][:], in_=xo_planes[:, j, :])
 
-        def load_weights(i):
-            a, b = spans[i]
+        def load_weights():
             for r in range(4):
                 nc.sync.dma_start(
-                    out=w_bytes[i][r:P:QUAD, :, :].bitcast(I32),
-                    in_=w_scales[a:b, 0, r:SCALE_ROWS:4, :].rearrange("e q n -> q e n").bitcast(I32),
+                    out=w_bytes[r:P:QUAD, :, :].bitcast(I32),
+                    in_=w_scales[:, 0, r:SCALE_ROWS:4, :].rearrange("e q n -> q e n").bitcast(I32),
                 )
-            for c, d in [(a, a + 1), (a + 1, b)] if i == 0 else [(a, b)]:
+            for i, (a, b) in enumerate(spans):
                 nc.sync.dma_start(
-                    out=w_codes[i][:, c - a : d - a, :].bitcast(I32),
-                    in_=w_words[c:d, 0, :, :].rearrange("e p b -> p e b").bitcast(I32),
+                    out=w_codes[i][:].bitcast(I32), in_=w_words[a:b, 0, :, :].rearrange("e p b -> p e b").bitcast(I32)
                 )
-            nc.sync.dma_start(out=gates[:, a * C : b * C], in_=gate[:, a * C : b * C])
 
         nc.sync.dma_start(out=far_words[:], in_=x_words[0].rearrange("p t d -> p (t d)").bitcast(I32))
         nc.sync.dma_start(far_list[:], offs2)
@@ -87,8 +81,8 @@ def tile_moe_loc_lin_silu_kernel(
             )
         load_plane(2)
         load_plane(3)
-        load_weights(0)
-        load_weights(1)
+        load_weights()
+        nc.sync.dma_start(out=gates[:], in_=gate)
 
         def multiply(dst, e, nb, token_codes, token_scales):
             i = 0 if e < EARLY else 1
@@ -96,160 +90,120 @@ def tile_moe_loc_lin_silu_kernel(
             nc.tensor.matmul_mx(
                 out=dst,
                 lhsT=w_codes[i][:, local, 2 * P * nb : 2 * P * (nb + 1)].bitcast(FP4X4),
-                lhsT_scale=w_bytes[i][:, local, P * nb : P * (nb + 1)],
+                lhsT_scale=w_bytes[:, e, P * nb : P * (nb + 1)],
                 rhs=token_codes.bitcast(FP8X4),
                 rhs_scale=token_scales,
                 start=True,
                 stop=True,
             )
 
-        far_codes, far_scales, far_out = {}, {}, {}
         out_rows = out.rearrange("(nb p) t -> p nb t", p=P)
+        far_codes = keep.tile([P, S], U32, name="far_codes", align_bytes=64)
+        far_scales = keep.tile([P, S], U8, name="far_scales", align_bytes=64)
+        far_out = [keep.tile([P, NB, PAIR], F32, name=f"far_out{i}", align_bytes=64) for i in range(GROUPS)]
 
-        def far_entries(a, b):
-            return far_list[:, a * C // ENTRIES : b * C // ENTRIES]
+        def gather_far(dst, src, a, b):
+            nc.vector.tensor_copy(dst[:, a:b], src.indirect(far_list[:, a // ENTRIES : b // ENTRIES]))
 
-        def gather_far_words(a, b):
-            tile = keep.tile([P, (b - a) * C], U32, name=f"far_codes{a}", align_bytes=64)
-            nc.vector.tensor_copy(tile[:], far_words[:].bitcast(U32).indirect(far_entries(a, b)))
-            for e in range(a, b):
-                far_codes[e] = tile[:, (e - a) * C : (e - a + 1) * C]
-
-        def gather_far_bytes(a, b, tag):
-            tile = keep.tile([P, (b - a) * C], U8, name=f"far_scales{a}", tag=tag, align_bytes=64)
-            nc.vector.tensor_copy(tile[:], far_bytes[:].indirect(far_entries(a, b)))
-            for e in range(a, b):
-                far_scales[e] = tile[:, (e - a) * C : (e - a + 1) * C]
-
-        def far_expert(e):
-            bank = psum.tile([P, NB, C], F32, name=f"far_bank{e}", tag=f"bank{FAR_BANKS[e]}")
+        def far_expert(e, b):
+            bank = psum.tile([P, NB, C], F32, name=f"far_bank{e}", tag=f"bank{b}")
+            cols = slice(e * C, (e + 1) * C)
             for nb in range(NB):
-                multiply(bank[:, nb, :], e, nb, far_codes[e], far_scales[e])
+                multiply(bank[:, nb, :], e, nb, far_codes[:, cols], far_scales[:, cols])
             i, second = divmod(e, 2)
-            if not second:
-                far_out[i] = keep.tile([P, NB, PAIR], F32, name=f"far_out{i}", tag=f"cast{i}", align_bytes=64)
             nc.scalar.activation(far_out[i][:, :, second * C : (second + 1) * C], bank[:], SILU)
             if second:
-                nc.scalar.dma_start(out=out_rows[:, :, T + i * PAIR : T + (i + 1) * PAIR], in_=far_out[i][:])
+                nc.sync.dma_start(out=out_rows[:, :, T + i * PAIR : T + (i + 1) * PAIR], in_=far_out[i][:])
 
-        rows, casts, banks, results = {}, {}, {}, {}
-        codes = [keep.tile([P, n], U32, name=f"codes{s}", tag=f"codes{s}", align_bytes=64) for s, n in GROUPS]
-        scales = [keep.tile([P, n], U8, name=f"scales{s}", tag=f"scales{s}", align_bytes=64) for s, n in GROUPS]
+        first = keep.tile([P, PACK, PAIR], BF16, name="first", align_bytes=64)
+        later = keep.tile([P, PACK, S - PAIR], BF16, name="later", align_bytes=64)
+        rows = [keep.tile([P, PAIR, PACK], BF16, name=f"rows{g}", align_bytes=64) for g in range(GROUPS)]
+        codes = [keep.tile([P, PAIR], U32, name=f"codes{g}", align_bytes=64) for g in range(GROUPS)]
+        scales = [keep.tile([P, PAIR], U8, name=f"scales{g}", align_bytes=64) for g in range(GROUPS)]
 
-        def own_entries(g):
-            s, n = GROUPS[g]
-            return own_list[:, s // ENTRIES : (s + n) // ENTRIES]
+        def own_entries(a, b):
+            return own_list[:, a // ENTRIES : b // ENTRIES]
 
-        def new_rows(g, tag):
-            s, n = GROUPS[g]
-            rows[g] = keep.tile([P, n, PACK], BF16, name=f"rows{s}", tag=tag, align_bytes=64)
+        def gather_first(j):
+            nc.vector.tensor_copy(first[:, j, :], planes[j][:].indirect(own_entries(0, PAIR)))
 
-        def cast(j, tag):
-            casts[j] = keep.tile([P, T], BF16, name=f"cast{j}", tag=tag, align_bytes=64)
-            nc.scalar.copy(casts[j][:], planes[j][:])
+        def gather_later(j):
+            nc.scalar.activation(later[:, j, :], planes[j][:].indirect(own_entries(PAIR, S)), COPY)
 
-        def gather_vector(g, j):
-            nc.vector.tensor_copy(rows[g][:, :, j], planes[j][:].indirect(own_entries(g)))
-
-        def gather_scalar(g, lo, hi):
-            for j in range(lo, hi):
-                nc.scalar.activation(rows[g][:, :, j], casts[j][:].indirect(own_entries(g)), COPY)
+        def interleave(g):
+            src = first[:] if g == 0 else later[:, :, (g - 1) * PAIR : g * PAIR]
+            nc.vector.tensor_copy(rows[g][:], src.rearrange("p j n -> p n j"))
 
         def quantize(g):
             nc.vector.quantize_mx(
                 out=codes[g][:].bitcast(FP8X4), scales=scales[g][:], in_=rows[g][:].rearrange("p n j -> p (n j)")
             )
 
-        def products(g, lo, hi, b):
-            s, n = GROUPS[g]
-            bank = psum.tile([P, hi - lo, n], F32, name=f"bank{g}_{lo}", tag=f"bank{b}")
-            for nb in range(lo, hi):
-                banks[g, nb] = (bank, lo)
-                for u in range(n // C):
+        def own_bank(parts, b, dst):
+            name = "_".join(f"{g}{nb}" for g, nb in parts)
+            bank = psum.tile([P, len(parts), PAIR], F32, name=f"own_bank{name}", tag=f"bank{b}")
+            for i, (g, nb) in enumerate(parts):
+                for u in range(PAIR // C):
                     cols = slice(u * C, (u + 1) * C)
-                    multiply(bank[:, nb - lo, cols], s // C + u, nb, codes[g][:, cols], scales[g][:, cols])
-
-        def silu(g, lo, hi):
-            n = GROUPS[g][1]
-            bank, first = banks[g, lo]
-            tile = keep.tile([P, hi - lo, n], F32, name=f"result{g}_{lo}", align_bytes=64)
-            nc.scalar.activation(tile[:], bank[:, lo - first : hi - first, :], SILU)
-            for nb in range(lo, hi):
-                results[g, nb] = tile[:, nb - lo, :]
-
-        def scatter(g, lo, hi):
-            s, n = GROUPS[g]
-            for nb in range(lo, hi):
-                nc.vector.tensor_tensor(
-                    windows[nb][:].indirect(own_entries(g)), results[g, nb], gates[:, s : s + n], MULT
-                )
-
-        gather_far_words(0, FAR_CUT)
-        gather_far_words(FAR_CUT, E)
-        gather_far_bytes(0, FAR_CUT, "far_scales0")
-        new_rows(0, "rows0")
-        new_rows(1, "rows1")
-        for j in range(PACK - 1):
-            cast(j, f"cast{j}")
-            gather_vector(0, j)
-        gather_scalar(1, 0, 2)
-        gather_vector(1, 2)
-        gather_vector(0, 3)
-        quantize(0)
-        gather_vector(1, 3)
-        gather_far_bytes(FAR_CUT, E, "rows0")
-        quantize(1)
-
-        products(0, 0, 1, 0)
-        silu(0, 0, 1)
-        products(0, 1, NB, 1)
-        silu(0, 1, NB)
-        products(1, 0, NB, 2)
-        silu(1, 0, 1)
-        scatter(0, 0, NB)
-        scatter(1, 0, 1)
-
-        cast(PACK - 1, "codes0")
-        new_rows(2, "scales0")
-        gather_scalar(2, 0, PACK)
-        quantize(2)
-        products(2, 0, NB, 3)
-        silu(1, 1, NB)
-        scatter(1, 1, NB)
-
-        new_rows(3, f"codes{GROUPS[1][0]}")
-        gather_scalar(3, 0, PACK - 1)
-        silu(2, 0, 1)
-        scatter(2, 0, 1)
-        gather_scalar(3, PACK - 1, PACK)
-        quantize(3)
-        products(3, 0, NB, 4)
-        silu(2, 1, NB)
-        scatter(2, 1, NB)
-
-        new_rows(4, f"codes{GROUPS[2][0]}")
-        gather_scalar(4, 0, 2)
-        silu(3, 0, 1)
-        scatter(3, 0, 1)
-        gather_scalar(4, 2, PACK)
-        quantize(4)
-        products(4, 0, 2, 5)
-        products(4, 2, NB, 6)
-        silu(3, 1, NB)
-        scatter(3, 1, NB)
-
-        for e in range(3):
-            far_expert(e)
-        silu(4, 0, 1)
-        far_expert(3)
-        far_expert(4)
-        silu(4, 1, 2)
-        far_expert(5)
-        silu(4, 2, NB)
-        for nb in range(NB):
-            scatter(4, nb, nb + 1)
-            if nb < NB - 1:
-                nc.sync.dma_start(out=out_rows[:, nb, 0:T], in_=windows[nb][:])
+                    multiply(bank[:, i, cols], 2 * g + u, nb, codes[g][:, cols], scales[g][:, cols])
+            if dst is None:
+                for i, (g, nb) in enumerate(parts):
+                    nc.scalar.activation(results[nb][:, g * PAIR : (g + 1) * PAIR], bank[:, i, :], SILU)
             else:
-                nc.sync.dma_start(out=out_rows[:, nb, 0 : T // 2], in_=windows[nb][:, 0 : T // 2])
-                nc.scalar.dma_start(out=out_rows[:, nb, T // 2 : T], in_=windows[nb][:, T // 2 : T])
+                nc.scalar.activation(dst, bank[:], SILU)
+
+        def gate_product(nb, a, b):
+            nc.vector.tensor_tensor(results[nb][:, a:b], results[nb][:, a:b], gates[:, a:b], MULT)
+
+        def scatter_vector(nb, a, b):
+            nc.vector.tensor_tensor(windows[nb][:].indirect(own_entries(a, b)), results[nb][:, a:b], gates[:, a:b], MULT)
+
+        def scatter_scalar(nb, a, b):
+            nc.scalar.activation(windows[nb][:].indirect(own_entries(a, b)), results[nb][:, a:b], COPY)
+
+        soon = {nb: keep.tile([P, S], F32, name=f"soon{nb}", align_bytes=64) for nb in (3, 0)}
+        late = keep.tile([P, 2 * GROUPS, PAIR], F32, name="late", align_bytes=64)
+        late_rows = late[:].rearrange("p (r g) n -> p r (g n)", r=2)
+        results = {3: soon[3][:], 0: soon[0][:], 2: late_rows[:, 0, :], 1: late_rows[:, 1, :]}
+
+        def late_bank(i, b):
+            parts = [(g, nb) for nb in (2, 1) for g in range(GROUPS)][2 * i : 2 * i + 2]
+            own_bank(parts, b, late[:, 2 * i : 2 * i + 2, :])
+
+        gather_far(far_codes, far_words[:].bitcast(U32), 0, S // 2)
+        gather_far(far_codes, far_words[:].bitcast(U32), S // 2, S)
+        for j in range(PACK):
+            gather_first(j)
+            gather_later(j)
+            if j == 1:
+                gather_far(far_scales, far_bytes[:], 0, S // 2)
+                gather_far(far_scales, far_bytes[:], S // 2, S)
+        interleave(1)
+        interleave(0)
+        quantize(1)
+        interleave(2)
+        quantize(0)
+        quantize(2)
+        for e in range(E):
+            far_expert(e, e)
+        own_bank([(1, 0), (1, 3)], 2, None)
+        scatter_vector(0, PAIR, 2 * PAIR)
+        own_bank([(0, 3), (2, 3)], 3, None)
+        gate_product(3, 0, S)
+        own_bank([(0, 0), (2, 0)], 4, None)
+        scatter_vector(0, 0, PAIR)
+        scatter_vector(0, 2 * PAIR, S)
+        nc.sync.dma_start(out=out_rows[:, 0, 0:T], in_=windows[0][:])
+        late_bank(0, 5)
+        late_bank(1, 2)
+        gate_product(2, 0, S)
+        late_bank(2, 3)
+        scatter_scalar(3, 0, S // 2)
+        scatter_scalar(3, S // 2, S)
+        nc.sync.dma_start(out=out_rows[:, 3, 0:T], in_=windows[3][:])
+        scatter_vector(1, 0, S)
+        nc.sync.dma_start(out=out_rows[:, 1, 0:T], in_=windows[1][:])
+        scatter_scalar(2, 0, S // 2)
+        scatter_scalar(2, S // 2, S)
+        nc.sync.dma_start(out=out_rows[:, 2, 0 : T // 2], in_=windows[2][:, 0 : T // 2])
+        nc.scalar.dma_start(out=out_rows[:, 2, T // 2 : T], in_=windows[2][:, T // 2 : T])

@@ -27,6 +27,7 @@ SCALE_ROWS = K // 32
 EARLY = 2
 PAIR = 2 * C
 GROUPS = S // PAIR
+SHARE = 128
 
 
 def tile_moe_loc_lin_silu_kernel(
@@ -70,17 +71,16 @@ def tile_moe_loc_lin_silu_kernel(
                     out=w_codes[i][:].bitcast(I32), in_=w_words[a:b, 0, :, :].rearrange("e p b -> p e b").bitcast(I32)
                 )
 
-        nc.sync.dma_start(out=far_words[:], in_=x_words[0].rearrange("p t d -> p (t d)").bitcast(I32))
         nc.sync.dma_start(far_list[:], offs2)
-        nc.sync.dma_start(own_list[:], offs)
         load_plane(0)
-        load_plane(1)
+        nc.sync.dma_start(own_list[:], offs)
         for r in range(4):
             nc.sync.dma_start(
                 out=far_bytes[r:P:QUAD, :].bitcast(I32), in_=x_scales[0, r:SCALE_ROWS:4, :].bitcast(I32)
             )
-        load_plane(2)
-        load_plane(3)
+        nc.sync.dma_start(out=far_words[:], in_=x_words[0].rearrange("p t d -> p (t d)").bitcast(I32))
+        for j in range(1, PACK):
+            load_plane(j)
         load_weights()
         nc.sync.dma_start(out=gates[:], in_=gate)
 
@@ -115,8 +115,7 @@ def tile_moe_loc_lin_silu_kernel(
             if second:
                 nc.sync.dma_start(out=out_rows[:, :, T + i * PAIR : T + (i + 1) * PAIR], in_=far_out[i][:])
 
-        first = keep.tile([P, PACK, PAIR], BF16, name="first", align_bytes=64)
-        later = keep.tile([P, PACK, S - PAIR], BF16, name="later", align_bytes=64)
+        picked = [keep.tile([P, PACK, PAIR], BF16, name=f"picked{g}", align_bytes=64) for g in range(GROUPS)]
         rows = [keep.tile([P, PAIR, PACK], BF16, name=f"rows{g}", align_bytes=64) for g in range(GROUPS)]
         codes = [keep.tile([P, PAIR], U32, name=f"codes{g}", align_bytes=64) for g in range(GROUPS)]
         scales = [keep.tile([P, PAIR], U8, name=f"scales{g}", align_bytes=64) for g in range(GROUPS)]
@@ -124,15 +123,18 @@ def tile_moe_loc_lin_silu_kernel(
         def own_entries(a, b):
             return own_list[:, a // ENTRIES : b // ENTRIES]
 
-        def gather_first(j):
-            nc.vector.tensor_copy(first[:, j, :], planes[j][:].indirect(own_entries(0, PAIR)))
-
-        def gather_later(j):
-            nc.scalar.activation(later[:, j, :], planes[j][:].indirect(own_entries(PAIR, S)), COPY)
+        def gather_own(g, j):
+            window = planes[j][:].indirect(own_entries(g * PAIR, (g + 1) * PAIR))
+            if g == 0 and j in (1, 2):
+                nc.vector.tensor_copy(picked[g][:, j, :], window)
+            else:
+                nc.scalar.activation(picked[g][:, j, :], window, COPY)
 
         def interleave(g):
-            src = first[:] if g == 0 else later[:, :, (g - 1) * PAIR : g * PAIR]
-            nc.vector.tensor_copy(rows[g][:], src.rearrange("p j n -> p n j"))
+            src = picked[g][:]
+            nc.vector.tensor_copy(
+                rows[g][:].rearrange("p (c i) j -> p c j i", i=4), src.rearrange("p j (c i) -> p c j i", i=4)
+            )
 
         def quantize(g):
             nc.vector.quantize_mx(
@@ -170,40 +172,42 @@ def tile_moe_loc_lin_silu_kernel(
             parts = [(g, nb) for nb in (2, 1) for g in range(GROUPS)][2 * i : 2 * i + 2]
             own_bank(parts, b, late[:, 2 * i : 2 * i + 2, :])
 
+        gather_far(far_scales, far_bytes[:], 0, S // 2)
+        gather_far(far_scales, far_bytes[:], S // 2, S)
         gather_far(far_codes, far_words[:].bitcast(U32), 0, S // 2)
         gather_far(far_codes, far_words[:].bitcast(U32), S // 2, S)
         for j in range(PACK):
-            gather_first(j)
-            gather_later(j)
-            if j == 1:
-                gather_far(far_scales, far_bytes[:], 0, S // 2)
-                gather_far(far_scales, far_bytes[:], S // 2, S)
-        interleave(1)
+            for g in range(GROUPS):
+                gather_own(g, j)
         interleave(0)
-        quantize(1)
-        interleave(2)
+        interleave(1)
         quantize(0)
+        interleave(2)
+        quantize(1)
         quantize(2)
-        for e in range(E):
+        for e in range(3):
             far_expert(e, e)
-        own_bank([(1, 0), (1, 3)], 2, None)
-        scatter_vector(0, PAIR, 2 * PAIR)
-        own_bank([(0, 3), (2, 3)], 3, None)
-        gate_product(3, 0, S)
-        own_bank([(0, 0), (2, 0)], 4, None)
+        own_bank([(0, 0), (0, 3)], 1, None)
         scatter_vector(0, 0, PAIR)
-        scatter_vector(0, 2 * PAIR, S)
+        far_expert(3, 3)
+        far_expert(4, 4)
+        own_bank([(1, 3), (2, 3)], 2, results[3][:, PAIR:S].rearrange("p (g n) -> p g n", g=2))
+        gate_product(3, 0, S)
+        own_bank([(1, 0), (2, 0)], 1, results[0][:, PAIR:S].rearrange("p (g n) -> p g n", g=2))
+        scatter_vector(0, PAIR, S)
         nc.sync.dma_start(out=out_rows[:, 0, 0:T], in_=windows[0][:])
-        late_bank(0, 5)
-        late_bank(1, 2)
-        gate_product(2, 0, S)
-        late_bank(2, 3)
+        far_expert(5, 5)
+        late_bank(0, 3)
+        late_bank(1, 4)
+        scatter_vector(2, 0, SHARE)
+        gate_product(2, SHARE, S)
         scatter_scalar(3, 0, S // 2)
+        late_bank(2, 5)
         scatter_scalar(3, S // 2, S)
         nc.sync.dma_start(out=out_rows[:, 3, 0:T], in_=windows[3][:])
         scatter_vector(1, 0, S)
         nc.sync.dma_start(out=out_rows[:, 1, 0:T], in_=windows[1][:])
-        scatter_scalar(2, 0, S // 2)
-        scatter_scalar(2, S // 2, S)
+        scatter_scalar(2, SHARE, (SHARE + S) // 2)
+        scatter_scalar(2, (SHARE + S) // 2, S)
         nc.sync.dma_start(out=out_rows[:, 2, 0 : T // 2], in_=windows[2][:, 0 : T // 2])
         nc.scalar.dma_start(out=out_rows[:, 2, T // 2 : T], in_=windows[2][:, T // 2 : T])

@@ -78,9 +78,10 @@ def tile_moe_loc_lin_silu_kernel(
             nc.sync.dma_start(
                 out=far_bytes[r:P:QUAD, :].bitcast(I32), in_=x_scales[0, r:SCALE_ROWS:4, :].bitcast(I32)
             )
+        load_plane(1)
         nc.sync.dma_start(out=far_words[:], in_=x_words[0].rearrange("p t d -> p (t d)").bitcast(I32))
-        for j in range(1, PACK):
-            load_plane(j)
+        load_plane(2)
+        load_plane(3)
         load_weights()
         nc.sync.dma_start(out=gates[:], in_=gate)
 
@@ -112,11 +113,17 @@ def tile_moe_loc_lin_silu_kernel(
                 multiply(bank[:, nb, :], e, nb, far_codes[:, cols], far_scales[:, cols])
             i, second = divmod(e, 2)
             nc.scalar.activation(far_out[i][:, :, second * C : (second + 1) * C], bank[:], SILU)
-            if second:
+            if e >= E - 2:
+                nc.sync.dma_start(
+                    out=out_rows[:, :, T + e * C : T + (e + 1) * C], in_=far_out[i][:, :, second * C : (second + 1) * C]
+                )
+            elif second:
                 nc.sync.dma_start(out=out_rows[:, :, T + i * PAIR : T + (i + 1) * PAIR], in_=far_out[i][:])
 
-        picked = [keep.tile([P, PACK, PAIR], BF16, name=f"picked{g}", align_bytes=64) for g in range(GROUPS)]
-        rows = [keep.tile([P, PAIR, PACK], BF16, name=f"rows{g}", align_bytes=64) for g in range(GROUPS)]
+        picked = [
+            keep.tile([P, PACK, PAIR], BF16, name=f"picked{g}", tag=f"picked{g}", align_bytes=64) for g in range(GROUPS)
+        ]
+        rows = {}
         codes = [keep.tile([P, PAIR], U32, name=f"codes{g}", align_bytes=64) for g in range(GROUPS)]
         scales = [keep.tile([P, PAIR], U8, name=f"scales{g}", align_bytes=64) for g in range(GROUPS)]
 
@@ -125,13 +132,15 @@ def tile_moe_loc_lin_silu_kernel(
 
         def gather_own(g, j):
             window = planes[j][:].indirect(own_entries(g * PAIR, (g + 1) * PAIR))
-            if g == 0 and j in (1, 2):
+            if g == GROUPS - 1 and j >= 1:
                 nc.vector.tensor_copy(picked[g][:, j, :], window)
             else:
                 nc.scalar.activation(picked[g][:, j, :], window, COPY)
 
         def interleave(g):
             src = picked[g][:]
+            tag = "picked0" if g == GROUPS - 1 else f"rows{g}"
+            rows[g] = keep.tile([P, PAIR, PACK], BF16, name=f"rows{g}", tag=tag, align_bytes=64)
             nc.vector.tensor_copy(
                 rows[g][:].rearrange("p (c i) j -> p c j i", i=4), src.rearrange("p j (c i) -> p c j i", i=4)
             )
@@ -190,13 +199,12 @@ def tile_moe_loc_lin_silu_kernel(
         own_bank([(0, 0), (0, 3)], 1, None)
         scatter_vector(0, 0, PAIR)
         far_expert(3, 3)
-        far_expert(4, 4)
         own_bank([(1, 3), (2, 3)], 2, results[3][:, PAIR:S].rearrange("p (g n) -> p g n", g=2))
         gate_product(3, 0, S)
         own_bank([(1, 0), (2, 0)], 1, results[0][:, PAIR:S].rearrange("p (g n) -> p g n", g=2))
+        far_expert(4, 4)
         scatter_vector(0, PAIR, S)
         nc.sync.dma_start(out=out_rows[:, 0, 0:T], in_=windows[0][:])
-        far_expert(5, 5)
         late_bank(0, 3)
         late_bank(1, 4)
         scatter_vector(2, 0, SHARE)
@@ -205,9 +213,10 @@ def tile_moe_loc_lin_silu_kernel(
         late_bank(2, 5)
         scatter_scalar(3, S // 2, S)
         nc.sync.dma_start(out=out_rows[:, 3, 0:T], in_=windows[3][:])
+        scatter_scalar(2, SHARE, (SHARE + S) // 2)
+        far_expert(5, 5)
         scatter_vector(1, 0, S)
         nc.sync.dma_start(out=out_rows[:, 1, 0:T], in_=windows[1][:])
-        scatter_scalar(2, SHARE, (SHARE + S) // 2)
         scatter_scalar(2, (SHARE + S) // 2, S)
         nc.sync.dma_start(out=out_rows[:, 2, 0 : T // 2], in_=windows[2][:, 0 : T // 2])
         nc.scalar.dma_start(out=out_rows[:, 2, T // 2 : T], in_=windows[2][:, T // 2 : T])

@@ -27,7 +27,7 @@ SCALE_ROWS = K // 32
 EARLY = 2
 PAIR = 2 * C
 GROUPS = S // PAIR
-SHARE = 128
+SHARE = 224
 
 
 def tile_moe_loc_lin_silu_kernel(
@@ -150,36 +150,30 @@ def tile_moe_loc_lin_silu_kernel(
                 out=codes[g][:].bitcast(FP8X4), scales=scales[g][:], in_=rows[g][:].rearrange("p n j -> p (n j)")
             )
 
-        def own_bank(parts, b, dst):
+        results = {nb: keep.tile([P, S], F32, name=f"result{nb}", align_bytes=64) for nb in range(NB)}
+
+        def own_bank(parts, b):
             name = "_".join(f"{g}{nb}" for g, nb in parts)
             bank = psum.tile([P, len(parts), PAIR], F32, name=f"own_bank{name}", tag=f"bank{b}")
             for i, (g, nb) in enumerate(parts):
                 for u in range(PAIR // C):
                     cols = slice(u * C, (u + 1) * C)
                     multiply(bank[:, i, cols], 2 * g + u, nb, codes[g][:, cols], scales[g][:, cols])
-            if dst is None:
+            (g, nb), (h, mb) = parts
+            if nb == mb:
+                nc.scalar.activation(results[nb][:, g * PAIR : (h + 1) * PAIR], bank[:].rearrange("p i n -> p (i n)"), SILU)
+            else:
                 for i, (g, nb) in enumerate(parts):
                     nc.scalar.activation(results[nb][:, g * PAIR : (g + 1) * PAIR], bank[:, i, :], SILU)
-            else:
-                nc.scalar.activation(dst, bank[:], SILU)
 
-        def gate_product(nb, a, b):
-            nc.vector.tensor_tensor(results[nb][:, a:b], results[nb][:, a:b], gates[:, a:b], MULT)
+        def gate_product(engine, nb, a, b):
+            engine.tensor_tensor(results[nb][:, a:b], results[nb][:, a:b], gates[:, a:b], MULT)
 
         def scatter_vector(nb, a, b):
-            nc.vector.tensor_tensor(windows[nb][:].indirect(own_entries(a, b)), results[nb][:, a:b], gates[:, a:b], MULT)
+            nc.vector.tensor_copy(windows[nb][:].indirect(own_entries(a, b)), results[nb][:, a:b])
 
         def scatter_scalar(nb, a, b):
             nc.scalar.activation(windows[nb][:].indirect(own_entries(a, b)), results[nb][:, a:b], COPY)
-
-        soon = {nb: keep.tile([P, S], F32, name=f"soon{nb}", align_bytes=64) for nb in (3, 0)}
-        late = keep.tile([P, 2 * GROUPS, PAIR], F32, name="late", align_bytes=64)
-        late_rows = late[:].rearrange("p (r g) n -> p r (g n)", r=2)
-        results = {3: soon[3][:], 0: soon[0][:], 2: late_rows[:, 0, :], 1: late_rows[:, 1, :]}
-
-        def late_bank(i, b):
-            parts = [(g, nb) for nb in (2, 1) for g in range(GROUPS)][2 * i : 2 * i + 2]
-            own_bank(parts, b, late[:, 2 * i : 2 * i + 2, :])
 
         gather_far(far_scales, far_bytes[:], 0, S // 2)
         gather_far(far_scales, far_bytes[:], S // 2, S)
@@ -193,30 +187,37 @@ def tile_moe_loc_lin_silu_kernel(
         quantize(0)
         interleave(2)
         quantize(1)
-        quantize(2)
         for e in range(3):
             far_expert(e, e)
-        own_bank([(0, 0), (0, 3)], 1, None)
+        own_bank([(0, 0), (0, 1)], 1)
+        gate_product(nc.vector, 0, 0, PAIR)
+        quantize(2)
+        gate_product(nc.vector, 1, 0, PAIR)
         scatter_vector(0, 0, PAIR)
+        scatter_vector(1, 0, PAIR)
         far_expert(3, 3)
-        own_bank([(1, 3), (2, 3)], 2, results[3][:, PAIR:S].rearrange("p (g n) -> p g n", g=2))
-        gate_product(3, 0, S)
-        own_bank([(1, 0), (2, 0)], 1, results[0][:, PAIR:S].rearrange("p (g n) -> p g n", g=2))
-        far_expert(4, 4)
+        own_bank([(0, 3), (1, 3)], 2)
+        gate_product(nc.gpsimd, 3, 0, S // 2)
+        own_bank([(1, 0), (2, 0)], 1)
+        gate_product(nc.gpsimd, 0, PAIR, S)
         scatter_vector(0, PAIR, S)
         nc.sync.dma_start(out=out_rows[:, 0, 0:T], in_=windows[0][:])
-        late_bank(0, 3)
-        late_bank(1, 4)
+        own_bank([(2, 3), (0, 2)], 3)
+        gate_product(nc.gpsimd, 3, S // 2, S)
+        gate_product(nc.gpsimd, 2, 0, PAIR)
         scatter_vector(2, 0, SHARE)
-        gate_product(2, SHARE, S)
+        own_bank([(1, 1), (2, 1)], 2)
+        gate_product(nc.gpsimd, 1, PAIR, S)
+        far_expert(4, 4)
         scatter_scalar(3, 0, S // 2)
-        late_bank(2, 5)
+        own_bank([(1, 2), (2, 2)], 5)
+        gate_product(nc.gpsimd, 2, PAIR, S)
         scatter_scalar(3, S // 2, S)
         nc.sync.dma_start(out=out_rows[:, 3, 0:T], in_=windows[3][:])
-        scatter_scalar(2, SHARE, (SHARE + S) // 2)
+        scatter_scalar(2, SHARE, 2 * PAIR)
         far_expert(5, 5)
-        scatter_vector(1, 0, S)
+        scatter_vector(1, PAIR, S)
         nc.sync.dma_start(out=out_rows[:, 1, 0:T], in_=windows[1][:])
-        scatter_scalar(2, (SHARE + S) // 2, S)
+        scatter_scalar(2, 2 * PAIR, S)
         nc.sync.dma_start(out=out_rows[:, 2, 0 : T // 2], in_=windows[2][:, 0 : T // 2])
         nc.scalar.dma_start(out=out_rows[:, 2, T // 2 : T], in_=windows[2][:, T // 2 : T])

@@ -27,7 +27,7 @@ SCALE_ROWS = K // 32
 EARLY = 2
 PAIR = 2 * C
 GROUPS = S // PAIR
-SHARE = 224
+SHARE = 192
 
 
 def tile_moe_loc_lin_silu_kernel(
@@ -43,8 +43,7 @@ def tile_moe_loc_lin_silu_kernel(
         far_words = keep.tile([P, Q], I32, name="far_words", align_bytes=64)
         far_bytes = keep.tile([P, Q], U8, name="far_bytes", align_bytes=64)
         planes = [keep.tile([P, T], F32, name=f"plane{j}", align_bytes=64) for j in range(PACK)]
-        spans = [(0, EARLY), (EARLY, E)]
-        w_codes = [keep.tile([P, b - a, 2 * N], U8, name=f"w_codes{a}", align_bytes=64) for a, b in spans]
+        w_codes = [keep.tile([P, 2, 2 * N], U8, name=f"w_codes{g}", align_bytes=64) for g in range(GROUPS)]
         w_bytes = keep.tile([P, E, N], U8, name="w_bytes", align_bytes=64)
         gates = keep.tile([P, S], F32, name="gates", align_bytes=64)
         windows = [keep.tile([P, T], F32, name=f"window{nb}", align_bytes=64) for nb in range(NB)]
@@ -60,16 +59,18 @@ def tile_moe_loc_lin_silu_kernel(
         def load_plane(j):
             nc.sync.dma_start(out=planes[j][:], in_=xo_planes[:, j, :])
 
-        def load_weights():
+        def load_w_scales(a, b):
             for r in range(4):
                 nc.sync.dma_start(
-                    out=w_bytes[r:P:QUAD, :, :].bitcast(I32),
-                    in_=w_scales[:, 0, r:SCALE_ROWS:4, :].rearrange("e q n -> q e n").bitcast(I32),
+                    out=w_bytes[r:P:QUAD, a:b, :].bitcast(I32),
+                    in_=w_scales[a:b, 0, r:SCALE_ROWS:4, :].rearrange("e q n -> q e n").bitcast(I32),
                 )
-            for i, (a, b) in enumerate(spans):
-                nc.sync.dma_start(
-                    out=w_codes[i][:].bitcast(I32), in_=w_words[a:b, 0, :, :].rearrange("e p b -> p e b").bitcast(I32)
-                )
+
+        def load_w_words(g):
+            nc.sync.dma_start(
+                out=w_codes[g][:].bitcast(I32),
+                in_=w_words[2 * g : 2 * g + 2, 0, :, :].rearrange("e p b -> p e b").bitcast(I32),
+            )
 
         nc.sync.dma_start(far_list[:], offs2)
         load_plane(0)
@@ -82,12 +83,14 @@ def tile_moe_loc_lin_silu_kernel(
         nc.sync.dma_start(out=far_words[:], in_=x_words[0].rearrange("p t d -> p (t d)").bitcast(I32))
         load_plane(2)
         load_plane(3)
-        load_weights()
+        load_w_scales(0, E)
+        load_w_words(0)
+        load_w_words(1)
         nc.sync.dma_start(out=gates[:], in_=gate)
+        load_w_words(2)
 
         def multiply(dst, e, nb, token_codes, token_scales):
-            i = 0 if e < EARLY else 1
-            local = e - spans[i][0]
+            i, local = divmod(e, 2)
             nc.tensor.matmul_mx(
                 out=dst,
                 lhsT=w_codes[i][:, local, 2 * P * nb : 2 * P * (nb + 1)].bitcast(FP4X4),
@@ -187,35 +190,35 @@ def tile_moe_loc_lin_silu_kernel(
         quantize(0)
         interleave(2)
         quantize(1)
-        for e in range(3):
+        for e in range(4):
             far_expert(e, e)
-        own_bank([(0, 0), (0, 1)], 1)
+        own_bank([(0, 0), (0, 1)], 0)
         gate_product(nc.vector, 0, 0, PAIR)
         quantize(2)
         gate_product(nc.vector, 1, 0, PAIR)
         scatter_vector(0, 0, PAIR)
         scatter_vector(1, 0, PAIR)
-        far_expert(3, 3)
-        own_bank([(0, 3), (1, 3)], 2)
+        own_bank([(0, 3), (1, 3)], 1)
         gate_product(nc.gpsimd, 3, 0, S // 2)
-        own_bank([(1, 0), (2, 0)], 1)
+        own_bank([(0, 2), (1, 2)], 4)
+        gate_product(nc.gpsimd, 2, 0, SHARE)
+        scatter_vector(2, 0, SHARE)
+        own_bank([(2, 3), (1, 0)], 5)
+        gate_product(nc.gpsimd, 3, S // 2, S)
+        own_bank([(2, 0), (1, 1)], 6)
         gate_product(nc.gpsimd, 0, PAIR, S)
         scatter_vector(0, PAIR, S)
-        nc.sync.dma_start(out=out_rows[:, 0, 0:T], in_=windows[0][:])
-        own_bank([(2, 3), (0, 2)], 3)
-        gate_product(nc.gpsimd, 3, S // 2, S)
-        gate_product(nc.gpsimd, 2, 0, PAIR)
-        scatter_vector(2, 0, SHARE)
-        own_bank([(1, 1), (2, 1)], 2)
-        gate_product(nc.gpsimd, 1, PAIR, S)
-        far_expert(4, 4)
+        gate_product(nc.gpsimd, 2, SHARE, 2 * PAIR)
+        far_expert(4, 1)
         scatter_scalar(3, 0, S // 2)
-        own_bank([(1, 2), (2, 2)], 5)
-        gate_product(nc.gpsimd, 2, PAIR, S)
+        own_bank([(2, 1), (2, 2)], 7)
+        gate_product(nc.gpsimd, 1, PAIR, S)
+        gate_product(nc.gpsimd, 2, 2 * PAIR, S)
         scatter_scalar(3, S // 2, S)
         nc.sync.dma_start(out=out_rows[:, 3, 0:T], in_=windows[3][:])
+        nc.sync.dma_start(out=out_rows[:, 0, 0:T], in_=windows[0][:])
         scatter_scalar(2, SHARE, 2 * PAIR)
-        far_expert(5, 5)
+        far_expert(5, 7)
         scatter_vector(1, PAIR, S)
         nc.sync.dma_start(out=out_rows[:, 1, 0:T], in_=windows[1][:])
         scatter_scalar(2, 2 * PAIR, S)

@@ -203,10 +203,10 @@ def tile_moe_loc_lin_silu_kernel(
         own_bank([(0, 2), (1, 2)], 4)
         gate_product(nc.gpsimd, 2, 0, SHARE)
         scatter_vector(2, 0, SHARE)
-        own_bank([(2, 3), (1, 0)], 5)
-        gate_product(nc.gpsimd, 3, S // 2, S)
-        own_bank([(2, 0), (1, 1)], 6)
+        own_bank([(1, 0), (2, 0)], 5)
         gate_product(nc.gpsimd, 0, PAIR, S)
+        own_bank([(2, 3), (1, 1)], 6)
+        gate_product(nc.gpsimd, 3, S // 2, S)
         scatter_vector(0, PAIR, S)
         gate_product(nc.gpsimd, 2, SHARE, 2 * PAIR)
         far_expert(4, 1)
@@ -220,7 +220,8 @@ def tile_moe_loc_lin_silu_kernel(
         scatter_scalar(2, SHARE, 2 * PAIR)
         far_expert(5, 7)
         scatter_vector(1, PAIR, S)
-        nc.sync.dma_start(out=out_rows[:, 1, 0:T], in_=windows[1][:])
+        nc.sync.dma_start(out=out_rows[:, 1, 0 : T // 2], in_=windows[1][:, 0 : T // 2])
+        nc.sync.dma_start(out=out_rows[:, 1, T // 2 : T], in_=windows[1][:, T // 2 : T])
         scatter_scalar(2, 2 * PAIR, S)
         nc.sync.dma_start(out=out_rows[:, 2, 0 : T // 2], in_=windows[2][:, 0 : T // 2])
         nc.scalar.dma_start(out=out_rows[:, 2, T // 2 : T], in_=windows[2][:, T // 2 : T])

@@ -27,7 +27,7 @@ SCALE_ROWS = K // 32
 EARLY = 2
 PAIR = 2 * C
 GROUPS = S // PAIR
-SHARE = 192
+SHARE = 288
 
 
 def tile_moe_loc_lin_silu_kernel(
@@ -72,21 +72,28 @@ def tile_moe_loc_lin_silu_kernel(
                 in_=w_words[2 * g : 2 * g + 2, 0, :, :].rearrange("e p b -> p e b").bitcast(I32),
             )
 
+        def load_x_scales():
+            for r in range(4):
+                nc.sync.dma_start(
+                    out=far_bytes[r:P:QUAD, :].bitcast(I32), in_=x_scales[0, r:SCALE_ROWS:4, :].bitcast(I32)
+                )
+
+        def load_x_words():
+            nc.sync.dma_start(out=far_words[:], in_=x_words[0].rearrange("p t d -> p (t d)").bitcast(I32))
+
         nc.sync.dma_start(far_list[:], offs2)
         load_plane(0)
         nc.sync.dma_start(own_list[:], offs)
-        for r in range(4):
-            nc.sync.dma_start(
-                out=far_bytes[r:P:QUAD, :].bitcast(I32), in_=x_scales[0, r:SCALE_ROWS:4, :].bitcast(I32)
-            )
+        load_x_scales()
         load_plane(1)
-        nc.sync.dma_start(out=far_words[:], in_=x_words[0].rearrange("p t d -> p (t d)").bitcast(I32))
+        load_x_words()
         load_plane(2)
         load_plane(3)
-        load_w_scales(0, E)
+        load_w_scales(0, EARLY)
         load_w_words(0)
         load_w_words(1)
         nc.sync.dma_start(out=gates[:], in_=gate)
+        load_w_scales(EARLY, E)
         load_w_words(2)
 
         def multiply(dst, e, nb, token_codes, token_scales):
@@ -190,35 +197,37 @@ def tile_moe_loc_lin_silu_kernel(
         quantize(0)
         interleave(2)
         quantize(1)
-        for e in range(4):
-            far_expert(e, e)
-        own_bank([(0, 0), (0, 1)], 0)
+        far_expert(0, 0)
+        far_expert(1, 1)
+        own_bank([(0, 0), (0, 1)], 2)
         gate_product(nc.vector, 0, 0, PAIR)
         quantize(2)
         gate_product(nc.vector, 1, 0, PAIR)
         scatter_vector(0, 0, PAIR)
         scatter_vector(1, 0, PAIR)
-        own_bank([(0, 3), (1, 3)], 1)
+        own_bank([(0, 3), (1, 3)], 3)
         gate_product(nc.gpsimd, 3, 0, S // 2)
-        own_bank([(0, 2), (1, 2)], 4)
+        far_expert(2, 2)
+        far_expert(3, 3)
+        own_bank([(0, 2), (1, 2)], 0)
         gate_product(nc.gpsimd, 2, 0, SHARE)
         scatter_vector(2, 0, SHARE)
-        own_bank([(1, 0), (2, 0)], 5)
+        own_bank([(1, 0), (2, 0)], 1)
         gate_product(nc.gpsimd, 0, PAIR, S)
-        own_bank([(2, 3), (1, 1)], 6)
+        own_bank([(2, 3), (1, 1)], 2)
         gate_product(nc.gpsimd, 3, S // 2, S)
         scatter_vector(0, PAIR, S)
         gate_product(nc.gpsimd, 2, SHARE, 2 * PAIR)
-        far_expert(4, 1)
+        far_expert(4, 3)
         scatter_scalar(3, 0, S // 2)
-        own_bank([(2, 1), (2, 2)], 7)
+        own_bank([(2, 1), (2, 2)], 0)
         gate_product(nc.gpsimd, 1, PAIR, S)
         gate_product(nc.gpsimd, 2, 2 * PAIR, S)
         scatter_scalar(3, S // 2, S)
         nc.sync.dma_start(out=out_rows[:, 3, 0:T], in_=windows[3][:])
         nc.sync.dma_start(out=out_rows[:, 0, 0:T], in_=windows[0][:])
         scatter_scalar(2, SHARE, 2 * PAIR)
-        far_expert(5, 7)
+        far_expert(5, 0)
         scatter_vector(1, PAIR, S)
         nc.sync.dma_start(out=out_rows[:, 1, 0 : T // 2], in_=windows[1][:, 0 : T // 2])
         nc.sync.dma_start(out=out_rows[:, 1, T // 2 : T], in_=windows[1][:, T // 2 : T])

@@ -49,9 +49,8 @@ def tile_moe_loc_lin_silu_kernel(
         windows = [keep.tile([P, T], F32, name=f"window{nb}", align_bytes=64) for nb in range(NB)]
 
         nc.gpsimd.memset(far_bytes[:].bitcast(I32), 0)
+        nc.vector.memset(windows[0][:], 0.0)
         nc.vector.memset(w_bytes[:].rearrange("p e n -> p (e n)").bitcast(I32), 0)
-        for nb in range(NB - 1):
-            nc.gpsimd.memset(windows[nb][:], 0.0)
         nc.scalar.activation(windows[NB - 1][:], windows[0][:], SILU)
 
         xo_planes = xo.rearrange("(p j) t -> p j t", j=PACK)
@@ -95,6 +94,8 @@ def tile_moe_loc_lin_silu_kernel(
         nc.sync.dma_start(out=gates[:], in_=gate)
         load_w_scales(EARLY, E)
         load_w_words(2)
+        for nb in (1, 2):
+            nc.sync.dma_start(out=windows[nb][:], in_=windows[NB - 1][:])
 
         def multiply(dst, e, nb, token_codes, token_scales):
             i, local = divmod(e, 2)

@@ -84,8 +84,8 @@ def tile_moe_loc_lin_silu_kernel(
         load_plane(0)
         nc.sync.dma_start(own_list[:], offs)
         load_x_scales()
-        load_plane(1)
         load_x_words()
+        load_plane(1)
         load_plane(2)
         load_plane(3)
         load_w_scales(0, EARLY)
@@ -112,7 +112,7 @@ def tile_moe_loc_lin_silu_kernel(
         out_rows = out.rearrange("(nb p) t -> p nb t", p=P)
         far_codes = keep.tile([P, S], U32, name="far_codes", align_bytes=64)
         far_scales = keep.tile([P, S], U8, name="far_scales", align_bytes=64)
-        far_out = [keep.tile([P, NB, PAIR], F32, name=f"far_out{i}", align_bytes=64) for i in range(GROUPS)]
+        far_out = [keep.tile([P, NB, PAIR], F32, name=f"far_out{i}", align_bytes=64) for i in range(GROUPS - 1)]
 
         def gather_far(dst, src, a, b):
             nc.vector.tensor_copy(dst[:, a:b], src.indirect(far_list[:, a // ENTRIES : b // ENTRIES]))
@@ -123,13 +123,15 @@ def tile_moe_loc_lin_silu_kernel(
             for nb in range(NB):
                 multiply(bank[:, nb, :], e, nb, far_codes[:, cols], far_scales[:, cols])
             i, second = divmod(e, 2)
-            nc.scalar.activation(far_out[i][:, :, second * C : (second + 1) * C], bank[:], SILU)
             if e >= E - 2:
-                nc.sync.dma_start(
-                    out=out_rows[:, :, T + e * C : T + (e + 1) * C], in_=far_out[i][:, :, second * C : (second + 1) * C]
-                )
-            elif second:
-                nc.sync.dma_start(out=out_rows[:, :, T + i * PAIR : T + (i + 1) * PAIR], in_=far_out[i][:])
+                tag = "result3" if second else "far_single"
+                single = keep.tile([P, NB, C], F32, name=f"far_single{e}", tag=tag, align_bytes=64)
+                nc.scalar.activation(single[:], bank[:], SILU)
+                nc.sync.dma_start(out=out_rows[:, :, T + e * C : T + (e + 1) * C], in_=single[:])
+            else:
+                nc.scalar.activation(far_out[i][:, :, second * C : (second + 1) * C], bank[:], SILU)
+                if second:
+                    nc.sync.dma_start(out=out_rows[:, :, T + i * PAIR : T + (i + 1) * PAIR], in_=far_out[i][:])
 
         picked = [
             keep.tile([P, PACK, PAIR], BF16, name=f"picked{g}", tag=f"picked{g}", align_bytes=64) for g in range(GROUPS)
@@ -141,12 +143,13 @@ def tile_moe_loc_lin_silu_kernel(
         def own_entries(a, b):
             return own_list[:, a // ENTRIES : b // ENTRIES]
 
-        def gather_own(g, j):
-            window = planes[j][:].indirect(own_entries(g * PAIR, (g + 1) * PAIR))
-            if g == GROUPS - 1 and j >= 1:
-                nc.vector.tensor_copy(picked[g][:, j, :], window)
+        def gather_own(engine, j, a, b):
+            window = planes[j][:].indirect(own_entries(a, b))
+            dst = picked[a // PAIR][:, j, a % PAIR : a % PAIR + b - a]
+            if engine is nc.vector:
+                nc.vector.tensor_copy(dst, window)
             else:
-                nc.scalar.activation(picked[g][:, j, :], window, COPY)
+                nc.scalar.activation(dst, window, COPY)
 
         def interleave(g):
             src = picked[g][:]
@@ -190,9 +193,13 @@ def tile_moe_loc_lin_silu_kernel(
         gather_far(far_scales, far_bytes[:], S // 2, S)
         gather_far(far_codes, far_words[:].bitcast(U32), 0, S // 2)
         gather_far(far_codes, far_words[:].bitcast(U32), S // 2, S)
-        for j in range(PACK):
+        for j in range(PACK - 1):
             for g in range(GROUPS):
-                gather_own(g, j)
+                gather_own(nc.vector if g == GROUPS - 1 and j >= 1 else nc.scalar, j, g * PAIR, (g + 1) * PAIR)
+        gather_own(nc.vector, PACK - 1, 0, C)
+        gather_own(nc.scalar, PACK - 1, C, PAIR)
+        gather_own(nc.scalar, PACK - 1, PAIR, 2 * PAIR)
+        gather_own(nc.scalar, PACK - 1, 2 * PAIR, S)
         interleave(0)
         interleave(1)
         quantize(0)
@@ -206,29 +213,29 @@ def tile_moe_loc_lin_silu_kernel(
         gate_product(nc.vector, 1, 0, PAIR)
         scatter_vector(0, 0, PAIR)
         scatter_vector(1, 0, PAIR)
-        own_bank([(0, 3), (1, 3)], 3)
-        gate_product(nc.gpsimd, 3, 0, S // 2)
+        own_bank([(0, 3), (0, 2)], 3)
+        gate_product(nc.gpsimd, 3, 0, PAIR)
+        own_bank([(1, 0), (2, 0)], 0)
+        gate_product(nc.gpsimd, 0, PAIR, S)
+        gate_product(nc.gpsimd, 2, 0, PAIR)
+        scatter_vector(0, PAIR, S)
+        nc.sync.dma_start(out=out_rows[:, 0, 0:T], in_=windows[0][:])
         far_expert(2, 2)
         far_expert(3, 3)
-        own_bank([(0, 2), (1, 2)], 0)
-        gate_product(nc.gpsimd, 2, 0, SHARE)
-        scatter_vector(2, 0, SHARE)
-        own_bank([(1, 0), (2, 0)], 1)
-        gate_product(nc.gpsimd, 0, PAIR, S)
-        own_bank([(2, 3), (1, 1)], 2)
+        own_bank([(1, 3), (2, 3)], 1)
+        gate_product(nc.gpsimd, 3, PAIR, S // 2)
         gate_product(nc.gpsimd, 3, S // 2, S)
-        scatter_vector(0, PAIR, S)
-        gate_product(nc.gpsimd, 2, SHARE, 2 * PAIR)
-        far_expert(4, 3)
-        scatter_scalar(3, 0, S // 2)
-        own_bank([(2, 1), (2, 2)], 0)
+        own_bank([(1, 2), (2, 2)], 0)
+        gate_product(nc.gpsimd, 2, PAIR, S)
+        scatter_vector(2, 0, SHARE)
+        own_bank([(1, 1), (2, 1)], 2)
         gate_product(nc.gpsimd, 1, PAIR, S)
-        gate_product(nc.gpsimd, 2, 2 * PAIR, S)
+        scatter_scalar(3, 0, S // 2)
+        far_expert(4, 3)
         scatter_scalar(3, S // 2, S)
         nc.sync.dma_start(out=out_rows[:, 3, 0:T], in_=windows[3][:])
-        nc.sync.dma_start(out=out_rows[:, 0, 0:T], in_=windows[0][:])
         scatter_scalar(2, SHARE, 2 * PAIR)
-        far_expert(5, 0)
+        far_expert(5, 1)
         scatter_vector(1, PAIR, S)
         nc.sync.dma_start(out=out_rows[:, 1, 0 : T // 2], in_=windows[1][:, 0 : T // 2])
         nc.sync.dma_start(out=out_rows[:, 1, T // 2 : T], in_=windows[1][:, T // 2 : T])

@@ -27,6 +27,7 @@ SCALE_ROWS = K // 32
 EARLY = 2
 PAIR = 2 * C
 GROUPS = S // PAIR
+FIRST = 64
 SHARE = 288
 
 
@@ -51,7 +52,8 @@ def tile_moe_loc_lin_silu_kernel(
         nc.gpsimd.memset(far_bytes[:].bitcast(I32), 0)
         nc.vector.memset(windows[0][:], 0.0)
         nc.vector.memset(w_bytes[:].rearrange("p e n -> p (e n)").bitcast(I32), 0)
-        nc.scalar.activation(windows[NB - 1][:], windows[0][:], SILU)
+        nc.vector.memset(windows[NB - 1][:, FIRST:T], 0.0)
+        nc.scalar.activation(windows[NB - 1][:, 0:FIRST], windows[0][:, 0:FIRST], SILU)
 
         xo_planes = xo.rearrange("(p j) t -> p j t", j=PACK)
 
@@ -84,8 +86,8 @@ def tile_moe_loc_lin_silu_kernel(
         load_plane(0)
         nc.sync.dma_start(own_list[:], offs)
         load_x_scales()
-        load_x_words()
         load_plane(1)
+        load_x_words()
         load_plane(2)
         load_plane(3)
         load_w_scales(0, EARLY)
@@ -193,13 +195,10 @@ def tile_moe_loc_lin_silu_kernel(
         gather_far(far_scales, far_bytes[:], S // 2, S)
         gather_far(far_codes, far_words[:].bitcast(U32), 0, S // 2)
         gather_far(far_codes, far_words[:].bitcast(U32), S // 2, S)
-        for j in range(PACK - 1):
+        for j in range(PACK):
             for g in range(GROUPS):
-                gather_own(nc.vector if g == GROUPS - 1 and j >= 1 else nc.scalar, j, g * PAIR, (g + 1) * PAIR)
-        gather_own(nc.vector, PACK - 1, 0, C)
-        gather_own(nc.scalar, PACK - 1, C, PAIR)
-        gather_own(nc.scalar, PACK - 1, PAIR, 2 * PAIR)
-        gather_own(nc.scalar, PACK - 1, 2 * PAIR, S)
+                on_vector = (j, g) in ((2, GROUPS - 1), (3, 0))
+                gather_own(nc.vector if on_vector else nc.scalar, j, g * PAIR, (g + 1) * PAIR)
         interleave(0)
         interleave(1)
         quantize(0)

@@ -28,7 +28,7 @@ EARLY = 2
 PAIR = 2 * C
 GROUPS = S // PAIR
 FIRST = 64
-SHARE = 288
+SHARE = 320
 
 
 def tile_moe_loc_lin_silu_kernel(
@@ -135,10 +135,17 @@ def tile_moe_loc_lin_silu_kernel(
                 if second:
                     nc.sync.dma_start(out=out_rows[:, :, T + i * PAIR : T + (i + 1) * PAIR], in_=far_out[i][:])
 
+        def far_first(banks):
+            for half, b in enumerate(banks):
+                bank = psum.tile([P, 2, C], F32, name=f"far_half{half}", tag=f"bank{b}")
+                for i in range(2):
+                    multiply(bank[:, i, :], 0, 2 * half + i, far_codes[:, 0:C], far_scales[:, 0:C])
+                nc.scalar.activation(far_out[0][:, 2 * half : 2 * half + 2, 0:C], bank[:], SILU)
+
         picked = [
             keep.tile([P, PACK, PAIR], BF16, name=f"picked{g}", tag=f"picked{g}", align_bytes=64) for g in range(GROUPS)
         ]
-        rows = {}
+        rows = [keep.tile([P, PAIR, PACK], BF16, name=f"rows{g}", align_bytes=64) for g in range(GROUPS)]
         codes = [keep.tile([P, PAIR], U32, name=f"codes{g}", align_bytes=64) for g in range(GROUPS)]
         scales = [keep.tile([P, PAIR], U8, name=f"scales{g}", align_bytes=64) for g in range(GROUPS)]
 
@@ -153,17 +160,17 @@ def tile_moe_loc_lin_silu_kernel(
             else:
                 nc.scalar.activation(dst, window, COPY)
 
-        def interleave(g):
-            src = picked[g][:]
-            tag = "picked0" if g == GROUPS - 1 else f"rows{g}"
-            rows[g] = keep.tile([P, PAIR, PACK], BF16, name=f"rows{g}", tag=tag, align_bytes=64)
+        def interleave(g, a, b):
             nc.vector.tensor_copy(
-                rows[g][:].rearrange("p (c i) j -> p c j i", i=4), src.rearrange("p j (c i) -> p c j i", i=4)
+                rows[g][:, a:b, :].rearrange("p (c i) j -> p c j i", i=4),
+                picked[g][:, :, a:b].rearrange("p j (c i) -> p c j i", i=4),
             )
 
-        def quantize(g):
+        def quantize(g, a, b):
             nc.vector.quantize_mx(
-                out=codes[g][:].bitcast(FP8X4), scales=scales[g][:], in_=rows[g][:].rearrange("p n j -> p (n j)")
+                out=codes[g][:, a:b].bitcast(FP8X4),
+                scales=scales[g][:, a:b],
+                in_=rows[g][:, a:b, :].rearrange("p n j -> p (n j)"),
             )
 
         results = {nb: keep.tile([P, S], F32, name=f"result{nb}", align_bytes=64) for nb in range(NB)}
@@ -182,11 +189,21 @@ def tile_moe_loc_lin_silu_kernel(
                 for i, (g, nb) in enumerate(parts):
                     nc.scalar.activation(results[nb][:, g * PAIR : (g + 1) * PAIR], bank[:, i, :], SILU)
 
+        gated1 = keep.tile([P, PAIR], F32, name="gated1", tag="rows1", align_bytes=64)
+
+        def product(nb, a, b):
+            return gated1[:, a:b] if nb == 1 and b <= PAIR else results[nb][:, a:b]
+
         def gate_product(engine, nb, a, b):
-            engine.tensor_tensor(results[nb][:, a:b], results[nb][:, a:b], gates[:, a:b], MULT)
+            engine.tensor_tensor(product(nb, a, b), results[nb][:, a:b], gates[:, a:b], MULT)
 
         def scatter_vector(nb, a, b):
-            nc.vector.tensor_copy(windows[nb][:].indirect(own_entries(a, b)), results[nb][:, a:b])
+            nc.vector.tensor_copy(windows[nb][:].indirect(own_entries(a, b)), product(nb, a, b))
+
+        def scatter_gated(nb, a, b):
+            nc.vector.tensor_tensor(
+                windows[nb][:].indirect(own_entries(a, b)), results[nb][:, a:b], gates[:, a:b], MULT
+            )
 
         def scatter_scalar(nb, a, b):
             nc.scalar.activation(windows[nb][:].indirect(own_entries(a, b)), results[nb][:, a:b], COPY)
@@ -195,40 +212,42 @@ def tile_moe_loc_lin_silu_kernel(
         gather_far(far_scales, far_bytes[:], S // 2, S)
         gather_far(far_codes, far_words[:].bitcast(U32), 0, S // 2)
         gather_far(far_codes, far_words[:].bitcast(U32), S // 2, S)
-        for j in range(PACK):
+        for j in range(PACK - 1):
             for g in range(GROUPS):
-                on_vector = (j, g) in ((2, GROUPS - 1), (3, 0))
-                gather_own(nc.vector if on_vector else nc.scalar, j, g * PAIR, (g + 1) * PAIR)
-        interleave(0)
-        interleave(1)
-        quantize(0)
-        interleave(2)
-        quantize(1)
-        far_expert(0, 0)
+                gather_own(nc.vector if (j, g) == (2, GROUPS - 1) else nc.scalar, j, g * PAIR, (g + 1) * PAIR)
+        for e in range(2):
+            gather_own(nc.vector, PACK - 1, e * C, (e + 1) * C)
+        for g in range(1, GROUPS):
+            gather_own(nc.scalar, PACK - 1, g * PAIR, (g + 1) * PAIR)
+        for step in (interleave, quantize):
+            step(0, 0, C)
+            step(0, C, PAIR)
+        interleave(1, 0, PAIR)
+        interleave(2, 0, PAIR)
+        quantize(1, 0, PAIR)
+        far_first((4, 0))
         far_expert(1, 1)
-        own_bank([(0, 0), (0, 1)], 2)
-        gate_product(nc.vector, 0, 0, PAIR)
-        quantize(2)
+        own_bank([(0, 1), (0, 0)], 2)
+        quantize(2, 0, PAIR)
         gate_product(nc.vector, 1, 0, PAIR)
-        scatter_vector(0, 0, PAIR)
+        scatter_gated(0, 0, PAIR)
         scatter_vector(1, 0, PAIR)
         own_bank([(0, 3), (0, 2)], 3)
-        gate_product(nc.gpsimd, 3, 0, PAIR)
         own_bank([(1, 0), (2, 0)], 0)
         gate_product(nc.gpsimd, 0, PAIR, S)
-        gate_product(nc.gpsimd, 2, 0, PAIR)
         scatter_vector(0, PAIR, S)
         nc.sync.dma_start(out=out_rows[:, 0, 0:T], in_=windows[0][:])
         far_expert(2, 2)
         far_expert(3, 3)
         own_bank([(1, 3), (2, 3)], 1)
-        gate_product(nc.gpsimd, 3, PAIR, S // 2)
-        gate_product(nc.gpsimd, 3, S // 2, S)
+        gate_product(nc.gpsimd, 3, 0, S // 2)
         own_bank([(1, 2), (2, 2)], 0)
-        gate_product(nc.gpsimd, 2, PAIR, S)
+        gate_product(nc.gpsimd, 2, 0, SHARE)
+        gate_product(nc.gpsimd, 3, S // 2, S)
         scatter_vector(2, 0, SHARE)
         own_bank([(1, 1), (2, 1)], 2)
         gate_product(nc.gpsimd, 1, PAIR, S)
+        gate_product(nc.gpsimd, 2, SHARE, S)
         scatter_scalar(3, 0, S // 2)
         far_expert(4, 3)
         scatter_scalar(3, S // 2, S)

@@ -28,7 +28,6 @@ EARLY = 2
 PAIR = 2 * C
 GROUPS = S // PAIR
 FIRST = 64
-SHARE = 320
 
 
 def tile_moe_loc_lin_silu_kernel(
@@ -115,6 +114,8 @@ def tile_moe_loc_lin_silu_kernel(
         far_codes = keep.tile([P, S], U32, name="far_codes", align_bytes=64)
         far_scales = keep.tile([P, S], U8, name="far_scales", align_bytes=64)
         far_out = [keep.tile([P, NB, PAIR], F32, name=f"far_out{i}", align_bytes=64) for i in range(GROUPS - 1)]
+        far_single = keep.tile([P, NB, C], F32, name="far_single", align_bytes=64)
+        lanes = keep.tile([P, NB + 1, S], F32, name="lanes", align_bytes=64)
 
         def gather_far(dst, src, a, b):
             nc.vector.tensor_copy(dst[:, a:b], src.indirect(far_list[:, a // ENTRIES : b // ENTRIES]))
@@ -126,25 +127,15 @@ def tile_moe_loc_lin_silu_kernel(
                 multiply(bank[:, nb, :], e, nb, far_codes[:, cols], far_scales[:, cols])
             i, second = divmod(e, 2)
             if e >= E - 2:
-                tag = "result3" if second else "far_single"
-                single = keep.tile([P, NB, C], F32, name=f"far_single{e}", tag=tag, align_bytes=64)
-                nc.scalar.activation(single[:], bank[:], SILU)
-                nc.sync.dma_start(out=out_rows[:, :, T + e * C : T + (e + 1) * C], in_=single[:])
+                single = lanes[:, 0, S - N : S].rearrange("p (nb c) -> p nb c", c=C) if second else far_single[:]
+                nc.scalar.activation(single, bank[:], SILU)
+                nc.sync.dma_start(out=out_rows[:, :, T + e * C : T + (e + 1) * C], in_=single)
             else:
                 nc.scalar.activation(far_out[i][:, :, second * C : (second + 1) * C], bank[:], SILU)
                 if second:
                     nc.sync.dma_start(out=out_rows[:, :, T + i * PAIR : T + (i + 1) * PAIR], in_=far_out[i][:])
 
-        def far_first(banks):
-            for half, b in enumerate(banks):
-                bank = psum.tile([P, 2, C], F32, name=f"far_half{half}", tag=f"bank{b}")
-                for i in range(2):
-                    multiply(bank[:, i, :], 0, 2 * half + i, far_codes[:, 0:C], far_scales[:, 0:C])
-                nc.scalar.activation(far_out[0][:, 2 * half : 2 * half + 2, 0:C], bank[:], SILU)
-
-        picked = [
-            keep.tile([P, PACK, PAIR], BF16, name=f"picked{g}", tag=f"picked{g}", align_bytes=64) for g in range(GROUPS)
-        ]
+        picked = keep.tile([P, PACK, S], BF16, name="picked", align_bytes=64)
         rows = [keep.tile([P, PAIR, PACK], BF16, name=f"rows{g}", align_bytes=64) for g in range(GROUPS)]
         codes = [keep.tile([P, PAIR], U32, name=f"codes{g}", align_bytes=64) for g in range(GROUPS)]
         scales = [keep.tile([P, PAIR], U8, name=f"scales{g}", align_bytes=64) for g in range(GROUPS)]
@@ -154,7 +145,7 @@ def tile_moe_loc_lin_silu_kernel(
 
         def gather_own(engine, j, a, b):
             window = planes[j][:].indirect(own_entries(a, b))
-            dst = picked[a // PAIR][:, j, a % PAIR : a % PAIR + b - a]
+            dst = picked[:, j, a:b]
             if engine is nc.vector:
                 nc.vector.tensor_copy(dst, window)
             else:
@@ -163,7 +154,7 @@ def tile_moe_loc_lin_silu_kernel(
         def interleave(g, a, b):
             nc.vector.tensor_copy(
                 rows[g][:, a:b, :].rearrange("p (c i) j -> p c j i", i=4),
-                picked[g][:, :, a:b].rearrange("p j (c i) -> p c j i", i=4),
+                picked[:, :, g * PAIR + a : g * PAIR + b].rearrange("p j (c i) -> p c j i", i=4),
             )
 
         def quantize(g, a, b):
@@ -173,48 +164,46 @@ def tile_moe_loc_lin_silu_kernel(
                 in_=rows[g][:, a:b, :].rearrange("p n j -> p (n j)"),
             )
 
-        results = {nb: keep.tile([P, S], F32, name=f"result{nb}", align_bytes=64) for nb in range(NB)}
+        def result(nb, a, b):
+            return lanes[:, 0 if (nb, a) == (0, 0) else nb + 1, a:b]
 
-        def own_bank(parts, b):
+        def own_bank(parts, dst, b):
             name = "_".join(f"{g}{nb}" for g, nb in parts)
-            bank = psum.tile([P, len(parts), PAIR], F32, name=f"own_bank{name}", tag=f"bank{b}")
+            bank = psum.tile([P, 2, PAIR], F32, name=f"own_bank{name}", tag=f"bank{b}")
             for i, (g, nb) in enumerate(parts):
                 for u in range(PAIR // C):
                     cols = slice(u * C, (u + 1) * C)
                     multiply(bank[:, i, cols], 2 * g + u, nb, codes[g][:, cols], scales[g][:, cols])
-            (g, nb), (h, mb) = parts
-            if nb == mb:
-                nc.scalar.activation(results[nb][:, g * PAIR : (h + 1) * PAIR], bank[:].rearrange("p i n -> p (i n)"), SILU)
-            else:
-                for i, (g, nb) in enumerate(parts):
-                    nc.scalar.activation(results[nb][:, g * PAIR : (g + 1) * PAIR], bank[:, i, :], SILU)
+            nc.scalar.activation(dst, bank[:], SILU)
 
-        gated1 = keep.tile([P, PAIR], F32, name="gated1", tag="rows1", align_bytes=64)
+        def late_bank(nb, b):
+            own_bank([(1, nb), (2, nb)], result(nb, PAIR, S).rearrange("p (i n) -> p i n", i=2), b)
+
+        gated = [keep.tile([P, PAIR], F32, name=f"gated{nb}", tag=f"rows{nb + 1}", align_bytes=64) for nb in range(2)]
 
         def product(nb, a, b):
-            return gated1[:, a:b] if nb == 1 and b <= PAIR else results[nb][:, a:b]
+            if nb == 3:
+                return lanes[:, 0, a:b]
+            if b > PAIR:
+                return result(nb, a, b)
+            return result(1, a, b) if nb == 2 else gated[nb][:, a:b]
 
         def gate_product(engine, nb, a, b):
-            engine.tensor_tensor(product(nb, a, b), results[nb][:, a:b], gates[:, a:b], MULT)
+            engine.tensor_tensor(product(nb, a, b), result(nb, a, b), gates[:, a:b], MULT)
 
         def scatter_vector(nb, a, b):
             nc.vector.tensor_copy(windows[nb][:].indirect(own_entries(a, b)), product(nb, a, b))
 
-        def scatter_gated(nb, a, b):
-            nc.vector.tensor_tensor(
-                windows[nb][:].indirect(own_entries(a, b)), results[nb][:, a:b], gates[:, a:b], MULT
-            )
-
         def scatter_scalar(nb, a, b):
-            nc.scalar.activation(windows[nb][:].indirect(own_entries(a, b)), results[nb][:, a:b], COPY)
+            nc.scalar.activation(windows[nb][:].indirect(own_entries(a, b)), product(nb, a, b), COPY)
 
         gather_far(far_scales, far_bytes[:], 0, S // 2)
         gather_far(far_scales, far_bytes[:], S // 2, S)
         gather_far(far_codes, far_words[:].bitcast(U32), 0, S // 2)
         gather_far(far_codes, far_words[:].bitcast(U32), S // 2, S)
         for j in range(PACK - 1):
-            for g in range(GROUPS):
-                gather_own(nc.vector if (j, g) == (2, GROUPS - 1) else nc.scalar, j, g * PAIR, (g + 1) * PAIR)
+            gather_own(nc.scalar, j, 0, 2 * PAIR)
+            gather_own(nc.vector if j == 2 else nc.scalar, j, 2 * PAIR, S)
         for e in range(2):
             gather_own(nc.vector, PACK - 1, e * C, (e + 1) * C)
         for g in range(1, GROUPS):
@@ -225,35 +214,37 @@ def tile_moe_loc_lin_silu_kernel(
         interleave(1, 0, PAIR)
         interleave(2, 0, PAIR)
         quantize(1, 0, PAIR)
-        far_first((4, 0))
+        far_expert(0, 0)
         far_expert(1, 1)
-        own_bank([(0, 1), (0, 0)], 2)
+        own_bank([(0, 0), (0, 1)], lanes[:, 0:3:2, 0:PAIR], 2)
         quantize(2, 0, PAIR)
+        gate_product(nc.vector, 0, 0, PAIR)
         gate_product(nc.vector, 1, 0, PAIR)
-        scatter_gated(0, 0, PAIR)
+        scatter_vector(0, 0, PAIR)
         scatter_vector(1, 0, PAIR)
-        own_bank([(0, 3), (0, 2)], 3)
-        own_bank([(1, 0), (2, 0)], 0)
+        own_bank([(0, 2), (0, 3)], lanes[:, 3:5, 0:PAIR], 3)
+        gate_product(nc.gpsimd, 3, 0, PAIR)
+        gate_product(nc.gpsimd, 2, 0, PAIR)
+        scatter_vector(2, 0, PAIR)
+        far_expert(2, 0)
+        far_expert(3, 1)
+        late_bank(3, 2)
+        gate_product(nc.gpsimd, 3, PAIR, S // 2)
+        gate_product(nc.gpsimd, 3, S // 2, S)
+        late_bank(0, 3)
         gate_product(nc.gpsimd, 0, PAIR, S)
         scatter_vector(0, PAIR, S)
         nc.sync.dma_start(out=out_rows[:, 0, 0:T], in_=windows[0][:])
-        far_expert(2, 2)
-        far_expert(3, 3)
-        own_bank([(1, 3), (2, 3)], 1)
-        gate_product(nc.gpsimd, 3, 0, S // 2)
-        own_bank([(1, 2), (2, 2)], 0)
-        gate_product(nc.gpsimd, 2, 0, SHARE)
-        gate_product(nc.gpsimd, 3, S // 2, S)
-        scatter_vector(2, 0, SHARE)
-        own_bank([(1, 1), (2, 1)], 2)
-        gate_product(nc.gpsimd, 1, PAIR, S)
-        gate_product(nc.gpsimd, 2, SHARE, S)
+        far_expert(4, 0)
+        late_bank(2, 1)
+        gate_product(nc.gpsimd, 2, PAIR, S)
         scatter_scalar(3, 0, S // 2)
-        far_expert(4, 3)
+        late_bank(1, 2)
+        gate_product(nc.gpsimd, 1, PAIR, S)
         scatter_scalar(3, S // 2, S)
         nc.sync.dma_start(out=out_rows[:, 3, 0:T], in_=windows[3][:])
-        scatter_scalar(2, SHARE, 2 * PAIR)
-        far_expert(5, 1)
+        scatter_scalar(2, PAIR, 2 * PAIR)
+        far_expert(5, 3)
         scatter_vector(1, PAIR, S)
         nc.sync.dma_start(out=out_rows[:, 1, 0 : T // 2], in_=windows[1][:, 0 : T // 2])
         nc.sync.dma_start(out=out_rows[:, 1, T // 2 : T], in_=windows[1][:, T // 2 : T])

@@ -27,6 +27,7 @@ SCALE_ROWS = K // 32
 EARLY = 2
 PAIR = 2 * C
 GROUPS = S // PAIR
+HELP = 64
 FIRST = 64
 
 
@@ -136,7 +137,7 @@ def tile_moe_loc_lin_silu_kernel(
                     nc.sync.dma_start(out=out_rows[:, :, T + i * PAIR : T + (i + 1) * PAIR], in_=far_out[i][:])
 
         picked = keep.tile([P, PACK, S], BF16, name="picked", align_bytes=64)
-        rows = [keep.tile([P, PAIR, PACK], BF16, name=f"rows{g}", align_bytes=64) for g in range(GROUPS)]
+        rows = {}
         codes = [keep.tile([P, PAIR], U32, name=f"codes{g}", align_bytes=64) for g in range(GROUPS)]
         scales = [keep.tile([P, PAIR], U8, name=f"scales{g}", align_bytes=64) for g in range(GROUPS)]
 
@@ -151,17 +152,19 @@ def tile_moe_loc_lin_silu_kernel(
             else:
                 nc.scalar.activation(dst, window, COPY)
 
-        def interleave(g, a, b):
+        def interleave(a, b, turn):
+            rows[a] = keep.tile([P, b - a, PACK], BF16, name=f"rows{a}", tag=f"turn{turn}", align_bytes=64)
             nc.vector.tensor_copy(
-                rows[g][:, a:b, :].rearrange("p (c i) j -> p c j i", i=4),
-                picked[:, :, g * PAIR + a : g * PAIR + b].rearrange("p j (c i) -> p c j i", i=4),
+                rows[a][:].rearrange("p (c i) j -> p c j i", i=4),
+                picked[:, :, a:b].rearrange("p j (c i) -> p c j i", i=4),
             )
 
-        def quantize(g, a, b):
+        def quantize(a, b):
+            g, cols = a // PAIR, slice(a % PAIR, a % PAIR + b - a)
             nc.vector.quantize_mx(
-                out=codes[g][:, a:b].bitcast(FP8X4),
-                scales=scales[g][:, a:b],
-                in_=rows[g][:, a:b, :].rearrange("p n j -> p (n j)"),
+                out=codes[g][:, cols].bitcast(FP8X4),
+                scales=scales[g][:, cols],
+                in_=rows[a][:].rearrange("p n j -> p (n j)"),
             )
 
         def result(nb, a, b):
@@ -179,7 +182,7 @@ def tile_moe_loc_lin_silu_kernel(
         def late_bank(nb, b):
             own_bank([(1, nb), (2, nb)], result(nb, PAIR, S).rearrange("p (i n) -> p i n", i=2), b)
 
-        gated = [keep.tile([P, PAIR], F32, name=f"gated{nb}", tag=f"rows{nb + 1}", align_bytes=64) for nb in range(2)]
+        gated = {}
 
         def product(nb, a, b):
             if nb == 3:
@@ -189,6 +192,8 @@ def tile_moe_loc_lin_silu_kernel(
             return result(1, a, b) if nb == 2 else gated[nb][:, a:b]
 
         def gate_product(engine, nb, a, b):
+            if engine is nc.vector:
+                gated[nb] = keep.tile([P, PAIR], F32, name=f"gated{nb}", tag=f"turn{nb}", align_bytes=64)
             engine.tensor_tensor(product(nb, a, b), result(nb, a, b), gates[:, a:b], MULT)
 
         def scatter_vector(nb, a, b):
@@ -201,23 +206,27 @@ def tile_moe_loc_lin_silu_kernel(
         gather_far(far_scales, far_bytes[:], S // 2, S)
         gather_far(far_codes, far_words[:].bitcast(U32), 0, S // 2)
         gather_far(far_codes, far_words[:].bitcast(U32), S // 2, S)
-        for j in range(PACK - 1):
+        gather_own(nc.scalar, 0, 0, 2 * PAIR)
+        gather_own(nc.scalar, 0, 2 * PAIR, S - HELP)
+        gather_own(nc.vector, 0, S - HELP, S)
+        for j in (1, 2):
             gather_own(nc.scalar, j, 0, 2 * PAIR)
             gather_own(nc.vector if j == 2 else nc.scalar, j, 2 * PAIR, S)
         for e in range(2):
             gather_own(nc.vector, PACK - 1, e * C, (e + 1) * C)
         for g in range(1, GROUPS):
             gather_own(nc.scalar, PACK - 1, g * PAIR, (g + 1) * PAIR)
-        for step in (interleave, quantize):
-            step(0, 0, C)
-            step(0, C, PAIR)
-        interleave(1, 0, PAIR)
-        interleave(2, 0, PAIR)
-        quantize(1, 0, PAIR)
+        interleave(0, C, 0)
+        interleave(C, PAIR, 1)
+        quantize(0, C)
+        quantize(C, PAIR)
+        interleave(PAIR, 2 * PAIR, 0)
+        interleave(2 * PAIR, S, 1)
+        quantize(PAIR, 2 * PAIR)
+        quantize(2 * PAIR, S)
         far_expert(0, 0)
         far_expert(1, 1)
         own_bank([(0, 0), (0, 1)], lanes[:, 0:3:2, 0:PAIR], 2)
-        quantize(2, 0, PAIR)
         gate_product(nc.vector, 0, 0, PAIR)
         gate_product(nc.vector, 1, 0, PAIR)
         scatter_vector(0, 0, PAIR)

@@ -82,9 +82,9 @@ def tile_moe_loc_lin_silu_kernel(
         def load_x_words():
             nc.sync.dma_start(out=far_words[:], in_=x_words[0].rearrange("p t d -> p (t d)").bitcast(I32))
 
-        nc.sync.dma_start(far_list[:], offs2)
-        load_plane(0)
         nc.sync.dma_start(own_list[:], offs)
+        load_plane(0)
+        nc.sync.dma_start(far_list[:], offs2)
         load_x_scales()
         load_plane(1)
         load_x_words()
@@ -115,7 +115,7 @@ def tile_moe_loc_lin_silu_kernel(
         far_codes = keep.tile([P, S], U32, name="far_codes", align_bytes=64)
         far_scales = keep.tile([P, S], U8, name="far_scales", align_bytes=64)
         far_out = [keep.tile([P, NB, PAIR], F32, name=f"far_out{i}", align_bytes=64) for i in range(GROUPS - 1)]
-        far_single = keep.tile([P, NB, C], F32, name="far_single", align_bytes=64)
+        far_single = keep.tile([P, 2, PAIR], F32, name="far_single", align_bytes=64)
         lanes = keep.tile([P, NB + 1, S], F32, name="lanes", align_bytes=64)
 
         def gather_far(dst, src, a, b):
@@ -127,14 +127,19 @@ def tile_moe_loc_lin_silu_kernel(
             for nb in range(NB):
                 multiply(bank[:, nb, :], e, nb, far_codes[:, cols], far_scales[:, cols])
             i, second = divmod(e, 2)
-            if e >= E - 2:
-                single = lanes[:, 0, S - N : S].rearrange("p (nb c) -> p nb c", c=C) if second else far_single[:]
-                nc.scalar.activation(single, bank[:], SILU)
-                nc.sync.dma_start(out=out_rows[:, :, T + e * C : T + (e + 1) * C], in_=single)
-            else:
-                nc.scalar.activation(far_out[i][:, :, second * C : (second + 1) * C], bank[:], SILU)
-                if second:
-                    nc.sync.dma_start(out=out_rows[:, :, T + i * PAIR : T + (i + 1) * PAIR], in_=far_out[i][:])
+            nc.scalar.activation(far_out[i][:, :, second * C : (second + 1) * C], bank[:], SILU)
+            if second:
+                nc.sync.dma_start(out=out_rows[:, :, T + i * PAIR : T + (i + 1) * PAIR], in_=far_out[i][:])
+
+        def far_last(half, dst, b):
+            bank = psum.tile([P, 2, PAIR], F32, name=f"far_last{half}", tag=f"bank{b}")
+            for e in (E - 2, E - 1):
+                cols = slice(e * C, (e + 1) * C)
+                for i in range(2):
+                    place = slice((e % 2) * C, (e % 2 + 1) * C)
+                    multiply(bank[:, i, place], e, 2 * half + i, far_codes[:, cols], far_scales[:, cols])
+            nc.scalar.activation(dst, bank[:], SILU)
+            nc.sync.dma_start(out=out_rows[:, 2 * half : 2 * half + 2, T + S - PAIR : T + S], in_=dst)
 
         picked = keep.tile([P, PACK, S], BF16, name="picked", align_bytes=64)
         rows = {}
@@ -244,7 +249,7 @@ def tile_moe_loc_lin_silu_kernel(
         gate_product(nc.gpsimd, 0, PAIR, S)
         scatter_vector(0, PAIR, S)
         nc.sync.dma_start(out=out_rows[:, 0, 0:T], in_=windows[0][:])
-        far_expert(4, 0)
+        far_last(0, far_single[:], 0)
         late_bank(2, 1)
         gate_product(nc.gpsimd, 2, PAIR, S)
         scatter_scalar(3, 0, S // 2)
@@ -252,11 +257,11 @@ def tile_moe_loc_lin_silu_kernel(
         gate_product(nc.gpsimd, 1, PAIR, S)
         scatter_scalar(3, S // 2, S)
         nc.sync.dma_start(out=out_rows[:, 3, 0:T], in_=windows[3][:])
-        scatter_scalar(2, PAIR, 2 * PAIR)
-        far_expert(5, 3)
+        scatter_scalar(2, PAIR, S // 2)
+        far_last(1, lanes[:, 0, S - N : S].rearrange("p (i n) -> p i n", i=2), 3)
         scatter_vector(1, PAIR, S)
         nc.sync.dma_start(out=out_rows[:, 1, 0 : T // 2], in_=windows[1][:, 0 : T // 2])
         nc.sync.dma_start(out=out_rows[:, 1, T // 2 : T], in_=windows[1][:, T // 2 : T])
-        scatter_scalar(2, 2 * PAIR, S)
+        scatter_scalar(2, S // 2, S)
         nc.sync.dma_start(out=out_rows[:, 2, 0 : T // 2], in_=windows[2][:, 0 : T // 2])
         nc.scalar.dma_start(out=out_rows[:, 2, T // 2 : T], in_=windows[2][:, T // 2 : T])

from contextlib import ExitStack

import concourse.mybir as mybir

K, T, Q, E, C, N = 512, 1024, 768, 6, 128, 512
S = E * C
FLOPS = 2 * K * N * 2 * S

F32 = mybir.dt.float32
BF16 = mybir.dt.bfloat16
I32 = mybir.dt.int32
U32 = mybir.dt.uint32
U16 = mybir.dt.uint16
U8 = mybir.dt.uint8
FP8X4 = mybir.dt.float8_e4m3fn_x4
FP4X4 = mybir.dt.float4_e2m1fn_x4
SILU = mybir.ActivationFunctionType.Silu
COPY = mybir.ActivationFunctionType.Copy
MULT = mybir.AluOpType.mult

P = 128
PACK = 4
NB = N // P
ENTRIES = 16
QUAD = 32
SCALE_ROWS = K // 32
EARLY = 2
PAIR = 2 * C
GROUPS = S // PAIR
HELP = 64
FIRST = 64


def tile_moe_loc_lin_silu_kernel(
    tc, x_words, x_scales, xo, w_words, w_scales, gate, offs, offs2, out
):
    nc = tc.nc
    with ExitStack() as ctx:
        keep = ctx.enter_context(tc.tile_pool(name="keep", bufs=1))
        psum = ctx.enter_context(tc.psum_pool(name="psum", bufs=1))

        own_list = keep.tile([P, S // ENTRIES], U16, name="own_list")
        far_list = keep.tile([P, S // ENTRIES], U16, name="far_list")
        far_words = keep.tile([P, Q], I32, name="far_words", align_bytes=64)
        far_bytes = keep.tile([P, Q], U8, name="far_bytes", align_bytes=64)
        planes = [keep.tile([P, T], F32, name=f"plane{j}", align_bytes=64) for j in range(PACK)]
        w_codes = [keep.tile([P, 2, 2 * N], U8, name=f"w_codes{g}", align_bytes=64) for g in range(GROUPS)]
        w_bytes = keep.tile([P, E, N], U8, name="w_bytes", align_bytes=64)
        gates = keep.tile([P, S], F32, name="gates", align_bytes=64)
        windows = [keep.tile([P, T], F32, name=f"window{nb}", align_bytes=64) for nb in range(NB)]

        nc.gpsimd.memset(far_bytes[:].bitcast(I32), 0)
        nc.vector.memset(windows[0][:], 0.0)
        nc.vector.memset(w_bytes[:].rearrange("p e n -> p (e n)").bitcast(I32), 0)
        nc.vector.memset(windows[NB - 1][:, FIRST:T], 0.0)
        nc.scalar.activation(windows[NB - 1][:, 0:FIRST], windows[0][:, 0:FIRST], SILU)

        xo_planes = xo.rearrange("(p j) t -> p j t", j=PACK)

        def load_plane(j):
            nc.sync.dma_start(out=planes[j][:], in_=xo_planes[:, j, :])

        def load_w_scales(a, b):
            for r in range(4):
                nc.sync.dma_start(
                    out=w_bytes[r:P:QUAD, a:b, :].bitcast(I32),
                    in_=w_scales[a:b, 0, r:SCALE_ROWS:4, :].rearrange("e q n -> q e n").bitcast(I32),
                )

        def load_w_words(g):
            nc.sync.dma_start(
                out=w_codes[g][:].bitcast(I32),
                in_=w_words[2 * g : 2 * g + 2, 0, :, :].rearrange("e p b -> p e b").bitcast(I32),
            )

        def load_x_scales():
            for r in range(4):
                nc.sync.dma_start(
                    out=far_bytes[r:P:QUAD, :].bitcast(I32), in_=x_scales[0, r:SCALE_ROWS:4, :].bitcast(I32)
                )

        def load_x_words():
            nc.sync.dma_start(out=far_words[:], in_=x_words[0].rearrange("p t d -> p (t d)").bitcast(I32))

        nc.sync.dma_start(own_list[:], offs)
        load_plane(0)
        nc.sync.dma_start(far_list[:], offs2)
        load_x_scales()
        load_plane(1)
        load_x_words()
        load_plane(2)
        load_plane(3)
        load_w_scales(0, EARLY)
        load_w_words(0)
        load_w_words(1)
        nc.sync.dma_start(out=gates[:], in_=gate)
        load_w_scales(EARLY, E)
        load_w_words(2)
        for nb in (1, 2):
            nc.sync.dma_start(out=windows[nb][:], in_=windows[NB - 1][:])

        def multiply(dst, e, nb, token_codes, token_scales):
            i, local = divmod(e, 2)
            nc.tensor.matmul_mx(
                out=dst,
                lhsT=w_codes[i][:, local, 2 * P * nb : 2 * P * (nb + 1)].bitcast(FP4X4),
                lhsT_scale=w_bytes[:, e, P * nb : P * (nb + 1)],
                rhs=token_codes.bitcast(FP8X4),
                rhs_scale=token_scales,
                start=True,
                stop=True,
            )

        out_rows = out.rearrange("(nb p) t -> p nb t", p=P)
        far_codes = keep.tile([P, S], U32, name="far_codes", align_bytes=64)
        far_scales = keep.tile([P, S], U8, name="far_scales", align_bytes=64)
        far_out = [keep.tile([P, NB, PAIR], F32, name=f"far_out{i}", align_bytes=64) for i in range(GROUPS - 1)]
        far_single = keep.tile([P, 2, PAIR], F32, name="far_single", align_bytes=64)
        lanes = keep.tile([P, NB + 1, S], F32, name="lanes", align_bytes=64)

        def gather_far(dst, src, a, b):
            nc.vector.tensor_copy(dst[:, a:b], src.indirect(far_list[:, a // ENTRIES : b // ENTRIES]))

        def far_expert(e, b):
            bank = psum.tile([P, NB, C], F32, name=f"far_bank{e}", tag=f"bank{b}")
            cols = slice(e * C, (e + 1) * C)
            for nb in range(NB):
                multiply(bank[:, nb, :], e, nb, far_codes[:, cols], far_scales[:, cols])
            i, second = divmod(e, 2)
            nc.scalar.activation(far_out[i][:, :, second * C : (second + 1) * C], bank[:], SILU)
            if second:
                nc.sync.dma_start(out=out_rows[:, :, T + i * PAIR : T + (i + 1) * PAIR], in_=far_out[i][:])

        def far_last(half, dst, b):
            bank = psum.tile([P, 2, PAIR], F32, name=f"far_last{half}", tag=f"bank{b}")
            for e in (E - 2, E - 1):
                cols = slice(e * C, (e + 1) * C)
                for i in range(2):
                    place = slice((e % 2) * C, (e % 2 + 1) * C)
                    multiply(bank[:, i, place], e, 2 * half + i, far_codes[:, cols], far_scales[:, cols])
            nc.scalar.activation(dst, bank[:], SILU)
            nc.sync.dma_start(out=out_rows[:, 2 * half : 2 * half + 2, T + S - PAIR : T + S], in_=dst)

        picked = keep.tile([P, PACK, S], BF16, name="picked", align_bytes=64)
        rows = {}
        codes = [keep.tile([P, PAIR], U32, name=f"codes{g}", align_bytes=64) for g in range(GROUPS)]
        scales = [keep.tile([P, PAIR], U8, name=f"scales{g}", align_bytes=64) for g in range(GROUPS)]

        def own_entries(a, b):
            return own_list[:, a // ENTRIES : b // ENTRIES]

        def gather_own(engine, j, a, b):
            window = planes[j][:].indirect(own_entries(a, b))
            dst = picked[:, j, a:b]
            if engine is nc.vector:
                nc.vector.tensor_copy(dst, window)
            else:
                nc.scalar.activation(dst, window, COPY)

        def interleave(a, b, turn):
            rows[a] = keep.tile([P, b - a, PACK], BF16, name=f"rows{a}", tag=f"turn{turn}", align_bytes=64)
            nc.vector.tensor_copy(
                rows[a][:].rearrange("p (c i) j -> p c j i", i=4),
                picked[:, :, a:b].rearrange("p j (c i) -> p c j i", i=4),
            )

        def quantize(a, b):
            g, cols = a // PAIR, slice(a % PAIR, a % PAIR + b - a)
            nc.vector.quantize_mx(
                out=codes[g][:, cols].bitcast(FP8X4),
                scales=scales[g][:, cols],
                in_=rows[a][:].rearrange("p n j -> p (n j)"),
            )

        def result(nb, a, b):
            return lanes[:, 0 if (nb, a) == (0, 0) else nb + 1, a:b]

        def own_bank(parts, dst, b):
            name = "_".join(f"{g}{nb}" for g, nb in parts)
            bank = psum.tile([P, 2, PAIR], F32, name=f"own_bank{name}", tag=f"bank{b}")
            for i, (g, nb) in enumerate(parts):
                for u in range(PAIR // C):
                    cols = slice(u * C, (u + 1) * C)
                    multiply(bank[:, i, cols], 2 * g + u, nb, codes[g][:, cols], scales[g][:, cols])
            nc.scalar.activation(dst, bank[:], SILU)

        def late_bank(nb, b):
            own_bank([(1, nb), (2, nb)], result(nb, PAIR, S).rearrange("p (i n) -> p i n", i=2), b)

        gated = {}

        def product(nb, a, b):
            if nb == 3:
                return lanes[:, 0, a:b]
            if b > PAIR:
                return result(nb, a, b)
            return result(1, a, b) if nb == 2 else gated[nb][:, a:b]

        def gate_product(engine, nb, a, b):
            if engine is nc.vector:
                gated[nb] = keep.tile([P, PAIR], F32, name=f"gated{nb}", tag=f"turn{nb}", align_bytes=64)
            engine.tensor_tensor(product(nb, a, b), result(nb, a, b), gates[:, a:b], MULT)

        def scatter_vector(nb, a, b):
            nc.vector.tensor_copy(windows[nb][:].indirect(own_entries(a, b)), product(nb, a, b))

        def scatter_scalar(nb, a, b):
            nc.scalar.activation(windows[nb][:].indirect(own_entries(a, b)), product(nb, a, b), COPY)

        gather_far(far_scales, far_bytes[:], 0, S // 2)
        gather_far(far_scales, far_bytes[:], S // 2, S)
        gather_far(far_codes, far_words[:].bitcast(U32), 0, S // 2)
        gather_far(far_codes, far_words[:].bitcast(U32), S // 2, S)
        gather_own(nc.scalar, 0, 0, 2 * PAIR)
        gather_own(nc.scalar, 0, 2 * PAIR, S - HELP)
        gather_own(nc.vector, 0, S - HELP, S)
        for j in (1, 2):
            gather_own(nc.scalar, j, 0, 2 * PAIR)
            gather_own(nc.vector if j == 2 else nc.scalar, j, 2 * PAIR, S)
        for e in range(2):
            gather_own(nc.vector, PACK - 1, e * C, (e + 1) * C)
        for g in range(1, GROUPS):
            gather_own(nc.scalar, PACK - 1, g * PAIR, (g + 1) * PAIR)
        interleave(0, C, 0)
        interleave(C, PAIR, 1)
        quantize(0, C)
        quantize(C, PAIR)
        interleave(PAIR, 2 * PAIR, 0)
        interleave(2 * PAIR, S, 1)
        quantize(PAIR, 2 * PAIR)
        quantize(2 * PAIR, S)
        far_expert(0, 0)
        far_expert(1, 1)
        own_bank([(0, 0), (0, 1)], lanes[:, 0:3:2, 0:PAIR], 2)
        gate_product(nc.vector, 0, 0, PAIR)
        gate_product(nc.vector, 1, 0, PAIR)
        scatter_vector(0, 0, PAIR)
        scatter_vector(1, 0, PAIR)
        own_bank([(0, 2), (0, 3)], lanes[:, 3:5, 0:PAIR], 3)
        gate_product(nc.gpsimd, 3, 0, PAIR)
        gate_product(nc.gpsimd, 2, 0, PAIR)
        scatter_vector(2, 0, PAIR)
        far_expert(2, 0)
        far_expert(3, 1)
        late_bank(3, 2)
        gate_product(nc.gpsimd, 3, PAIR, S // 2)
        gate_product(nc.gpsimd, 3, S // 2, S)
        late_bank(0, 3)
        gate_product(nc.gpsimd, 0, PAIR, S)
        scatter_vector(0, PAIR, S)
        nc.sync.dma_start(out=out_rows[:, 0, 0:T], in_=windows[0][:])
        far_last(0, far_single[:], 0)
        late_bank(2, 1)
        gate_product(nc.gpsimd, 2, PAIR, S)
        scatter_scalar(3, 0, S // 2)
        late_bank(1, 2)
        gate_product(nc.gpsimd, 1, PAIR, S)
        scatter_scalar(3, S // 2, S)
        nc.sync.dma_start(out=out_rows[:, 3, 0:T], in_=windows[3][:])
        scatter_scalar(2, PAIR, S // 2)
        far_last(1, lanes[:, 0, S - N : S].rearrange("p (i n) -> p i n", i=2), 3)
        scatter_vector(1, PAIR, S)
        nc.sync.dma_start(out=out_rows[:, 1, 0 : T // 2], in_=windows[1][:, 0 : T // 2])
        nc.sync.dma_start(out=out_rows[:, 1, T // 2 : T], in_=windows[1][:, T // 2 : T])
        scatter_scalar(2, S // 2, S)
        nc.sync.dma_start(out=out_rows[:, 2, 0 : T // 2], in_=windows[2][:, 0 : T // 2])
        nc.scalar.dma_start(out=out_rows[:, 2, T // 2 : T], in_=windows[2][:, T // 2 : T])
